import numpy as np
import ml_dtypes


def mxq(x, axis, fmt="e4m3"):
    dtype, down = {"e4m3": (ml_dtypes.float8_e4m3fn, 7), "e5m2": (ml_dtypes.float8_e5m2, 14)}[fmt]
    v = np.moveaxis(np.asarray(x, np.float32).astype(ml_dtypes.bfloat16).astype(np.float64), axis, -1)
    blocks = v.reshape(v.shape[:-1] + (-1, 32))
    amax = np.abs(blocks).max(-1, keepdims=True)
    byte = np.maximum(np.where(amax > 0, np.frexp(amax)[1] - 1 + 127, 0) - down, 1)
    scale = np.exp2(byte - 127.0)
    codes = (blocks / scale).astype(np.float32).astype(dtype).astype(np.float64)
    return np.moveaxis((codes * scale).reshape(v.shape), -1, axis)


WIDE = False


def mx_kscale(k):
    if not WIDE:
        return np.ones(k)
    levels = np.array([10, -10, 5, -5, 0])
    if k % 512:
        return np.exp2(np.random.permutation(np.resize(levels, k // 32))).repeat(32)
    a = np.empty((k // 512, 16))
    for p in range(k // 512):
        a[p, :8] = np.random.permutation(np.resize(levels, 8))
        for g in range(8):
            far = levels[np.abs(levels - a[p, g]) >= 10]
            a[p, g + 8] = far[np.random.randint(len(far))]
    return np.exp2(a.ravel()).repeat(32)


def f64(x):
    return np.asarray(x).astype(np.float64)


def striped(idx):
    return np.tile(np.asarray(idx).reshape(-1, 16).T, (8, 1)).astype(np.uint16)


def unstriped(offs):
    return offs[:16].T.reshape(-1).astype(np.int64)


B, N, T, D, DV, NQ = 2, 512, 2048, 512, 256, 256
PAGE = 32
CAP = 2.0


def setup_inputs():
    n = np.random.standard_normal
    pages = np.random.permutation(T // PAGE)[:B * N // PAGE]
    idx = (pages[:, None] * PAGE + np.arange(PAGE)[None, :]).reshape(-1)
    s = mx_kscale(D)[:, None]
    u = np.ones(T)
    u[idx] = mx_kscale(B * N)
    r = np.random.uniform(0.5, 2.0, T)
    k = n((D, T)) / s
    v = n((DV, T)) / (u * r)
    return {
        "qT": (n((B, D, NQ)) * s * (1.00 / np.sqrt(D))).astype(np.float32),
        "kT": k.astype(np.float32),
        "vT": v.astype(np.float32),
        "vs": np.tile(u * r, (128, 1)).astype(np.float32),
        "offs": striped(idx),
    }


def reference(qT, kT, vT, vs, offs):
    idx = unstriped(offs)
    k = f64(kT)
    v = f64(vT)
    pick = lambda x: x[:, idx].reshape(x.shape[0], B, N).transpose(1, 0, 2)
    q = f64(qT)
    score = mxq(q, 1, "e4m3").transpose(0, 2, 1) @ mxq(pick(k), 1, "e4m3")
    score = CAP * np.tanh(score / CAP)
    m = score.max(-1, keepdims=True)
    p = np.exp(score - m)
    total = p.sum(-1, keepdims=True)
    w = p * pick(f64(vs))[:, :1, :]
    y = mxq(w, 2, "e4m3") @ mxq(pick(v).transpose(0, 2, 1), 1, "e4m3")
    y = y / total
    return y

@@ -1,0 +1,272 @@
+from contextlib import ExitStack
+
+import concourse.mybir as mybir
+from concourse.masks import make_identity
+
+B, N, T, D, DV, NQ = 2, 512, 2048, 512, 256, 256
+P = 128
+PACK = 4
+CAP = 2.0
+QT = NQ // P
+VB = DV // P
+COLS = N // 16
+
+FLOPS = 2 * B * NQ * N * (D + DV)
+BYTES = 4 * (B * D * NQ + D * T + DV * T + T + B * NQ * DV) + 2 * P * B * COLS
+
+F32 = mybir.dt.float32
+BF16 = mybir.dt.bfloat16
+U32 = mybir.dt.uint32
+U16 = mybir.dt.uint16
+U8 = mybir.dt.uint8
+FP8X4 = mybir.dt.float8_e4m3fn_x4
+ACT = mybir.ActivationFunctionType
+ALU = mybir.AluOpType
+
+
+def tile_attend_gqa_cap_kernel(tc, qT, kT, vT, vs, offs, out):
+    nc = tc.nc
+    with ExitStack() as ctx:
+        keep = ctx.enter_context(tc.tile_pool(name="keep", bufs=1))
+        work = ctx.enter_context(tc.tile_pool(name="work", bufs=4))
+        psum = ctx.enter_context(tc.psum_pool(name="psum", bufs=2))
+
+        offsets = keep.tile([P, B * COLS], U16, name="offsets")
+        k_pool = [keep.tile([P, T], F32, name=f"k_pool{t}") for t in range(PACK)]
+        v_pool = [keep.tile([P, T], F32, name=f"v_pool{h}") for h in range(VB)]
+        q_raw = [keep.tile([P, PACK, NQ], F32, name=f"q_raw{b}") for b in range(B)]
+        vs_pool = keep.tile([P, T], F32, name="vs_pool")
+        vs_row = keep.tile([P, B * N], F32, name="vs_row")
+        vs_col = keep.tile([P, B, PACK], F32, name="vs_col")
+        ident = keep.tile([P, P], F32, name="ident")
+        warm = keep.tile([P, 1], F32, name="warm")
+        totals = keep.tile([P, B * QT], F32, name="totals")
+        inv = keep.tile([P, B * QT], F32, name="inv")
+        q_packed = [keep.tile([P, NQ, PACK], BF16, name=f"q_packed{b}", align_bytes=64) for b in range(B)]
+        q_codes = [keep.tile([P, NQ], U32, name=f"q_codes{b}", align_bytes=64) for b in range(B)]
+        q_scales = [keep.tile([P, NQ], U8, name=f"q_scales{b}", align_bytes=64) for b in range(B)]
+        k_rows_of = keep.tile([P, PACK, B * N], F32, name="k_rows_of")
+        k_packed = [keep.tile([P, N, PACK], BF16, name=f"k_packed{b}", align_bytes=64) for b in range(B)]
+        k_codes = [keep.tile([P, N], U32, name=f"k_codes{b}", align_bytes=64) for b in range(B)]
+        k_scales = [keep.tile([P, N], U8, name=f"k_scales{b}", align_bytes=64) for b in range(B)]
+        v_rows = [keep.tile([P, B * N], F32, name=f"v_rows{h}") for h in range(VB)]
+        v_packed = [keep.tile([P, DV, PACK], BF16, name=f"v_packed{b}", align_bytes=64) for b in range(B)]
+        v_codes = [keep.tile([P, DV], U32, name=f"v_codes{b}", align_bytes=64) for b in range(B)]
+        v_scales = [keep.tile([P, DV], U8, name=f"v_scales{b}", align_bytes=64) for b in range(B)]
+        units = [(b, m) for b in range(B) for m in range(QT)]
+        w_codes = {u: keep.tile([P, P], U32, name=f"w_codes{u[0]}{u[1]}", align_bytes=64) for u in units}
+        w_scales = {u: keep.tile([P, P], U8, name=f"w_scales{u[0]}{u[1]}", align_bytes=64) for u in units}
+        w_packed = {u: keep.tile([P, P, PACK], BF16, name=f"w_packed{u[0]}{u[1]}", align_bytes=64) for u in units}
+        th = {u: keep.tile([P, N], F32, name=f"th{u[0]}{u[1]}") for u in units}
+        low = {u: keep.tile([P, 1], F32, name=f"low{u[0]}{u[1]}") for u in units}
+        p = {u: keep.tile([P, PACK, P], F32, name=f"p{u[0]}{u[1]}") for u in units}
+        score, wt, vt, acc = {}, {}, {}, {}
+        over = {(0, 1): "v_pool0"}
+
+        def quant(codes, scales, packed):
+            nc.vector.quantize_mx(out=codes.bitcast(FP8X4), scales=scales, in_=packed.rearrange("p n j -> p (n j)"))
+
+        def interleave_q(copy, b):
+            copy(q_packed[b][:], q_raw[b][:].rearrange("p j n -> p n j"))
+
+        def quant_q(b):
+            quant(q_codes[b][:], q_scales[b][:], q_packed[b][:])
+
+        def gather_vs():
+            nc.vector.tensor_copy(vs_row[:], vs_pool[:].indirect(offsets[:]))
+
+        def turn_vs():
+            for b in range(B):
+                up = psum.tile([P, PACK, P], F32, name="turn", bufs=4)
+                for t in range(PACK):
+                    nc.tensor.transpose(up[:, t, :], vs_row[:, b * N + t : (b + 1) * N : PACK], ident[:])
+                nc.scalar.copy(vs_col[:, b, :], up[:, :, 0])
+
+        def gather_k(t):
+            nc.vector.tensor_copy(k_rows_of[:, t, :], k_pool[t][:].indirect(offsets[:]))
+
+        def gather_k_of(t, b):
+            nc.vector.tensor_copy(k_rows_of[:, t, b * N : (b + 1) * N], k_pool[t][:].indirect(offsets[:, b * COLS : (b + 1) * COLS]))
+
+        def interleave_k(copy, t, b):
+            copy(k_packed[b][:, :, t : t + 2], k_rows_of[:, t : t + 2, b * N : (b + 1) * N].rearrange("p j n -> p n j"))
+
+        def quant_k(b):
+            quant(k_codes[b][:], k_scales[b][:], k_packed[b][:])
+
+        def scores(b, m):
+            cols = slice(m * P, (m + 1) * P)
+            s = psum.tile([P, N], F32, name="score", bufs=2)
+            score[b, m] = s
+            nc.tensor.matmul_mx(
+                out=s[:],
+                lhsT=q_codes[b][:, cols].bitcast(FP8X4),
+                lhsT_scale=q_scales[b][:, cols],
+                rhs=k_codes[b][:].bitcast(FP8X4),
+                rhs_scale=k_scales[b][:],
+                start=True,
+                stop=True,
+            )
+
+        def squash(*u):
+            nc.scalar.activation(th[u][:], score[u][:], ACT.Tanh, scale=1.0 / CAP)
+
+        def lowest(*u):
+            if u in over:
+                neg = keep.tile([P, N], F32, name=f"neg{u[0]}{u[1]}", tag=over[u])
+            else:
+                neg = work.tile([P, N], F32, name="neg")
+            nc.vector.tensor_scalar(neg[:], th[u][:], -CAP, None, op0=ALU.mult, op1=ALU.min, accum_out=low[u][:])
+
+        def expo(*u):
+            i = units.index(u)
+            nc.scalar.activation(
+                p[u][:].rearrange("q t s -> q s t"),
+                th[u][:].rearrange("q (s t) -> q s t", t=PACK),
+                ACT.Exp,
+                bias=low[u][:],
+                scale=CAP,
+                accum_out=totals[:, i : i + 1],
+            )
+
+        def turn_w(*u):
+            x = psum.tile([P, PACK, P], F32, name="turn", bufs=4)
+            wt[u] = x
+            for t in range(PACK):
+                nc.tensor.transpose(x[:, t, :], p[u][:, t, :], ident[:])
+
+        def weigh(*u):
+            nc.vector.tensor_tensor(
+                w_packed[u][:],
+                wt[u][:].rearrange("p t q -> p q t"),
+                vs_col[:, u[0], :].unsqueeze(1).to_broadcast([P, P, PACK]),
+                ALU.mult,
+            )
+
+        def quant_w(*u):
+            quant(w_codes[u][:], w_scales[u][:], w_packed[u][:])
+
+        def gather_v(h):
+            nc.vector.tensor_copy(v_rows[h][:], v_pool[h][:].indirect(offsets[:]))
+
+        def turn_v(h, b):
+            x = psum.tile([P, PACK, P], F32, name="turn", bufs=4)
+            vt[h, b] = x
+            for t in range(PACK):
+                nc.tensor.transpose(x[:, t, :], v_rows[h][:, b * N + t : (b + 1) * N : PACK], ident[:])
+
+        def pack_v(copy, h, b):
+            copy(v_packed[b][:, h * P : (h + 1) * P, :], vt[h, b][:].rearrange("p t e -> p e t"))
+
+        def quant_v(b):
+            quant(v_codes[b][:], v_scales[b][:], v_packed[b][:])
+
+        def product(*u):
+            b = u[0]
+            y = psum.tile([P, DV], F32, name="y", bufs=2)
+            acc[u] = y
+            nc.tensor.matmul_mx(
+                out=y[:],
+                lhsT=w_codes[u][:].bitcast(FP8X4),
+                lhsT_scale=w_scales[u][:],
+                rhs=v_codes[b][:].bitcast(FP8X4),
+                rhs_scale=v_scales[b][:],
+                start=True,
+                stop=True,
+            )
+
+        def finish(b, m, scalar):
+            u = (b, m)
+            i = units.index(u)
+            y = acc[u]
+            res = work.tile([P, DV], F32, name="res")
+            if scalar:
+                nc.scalar.activation(res[:], y[:], ACT.Copy, scale=inv[:, i : i + 1])
+            else:
+                nc.vector.tensor_scalar(res[:], y[:], inv[:, i : i + 1], None, op0=ALU.mult)
+            nc.sync.dma_start(out[b, m * P : (m + 1) * P, :], res[:])
+
+        nc.gpsimd.memset(vs_pool[:, T // 2 : T], 0.0)
+        nc.vector.memset(vs_pool[:, 0 : T // 2], 0.0)
+        nc.sync.dma_start(offsets[:], offs)
+        k_rows = kT.rearrange("(p j) n -> j p n", j=PACK)
+        q_rows = [qT[b].rearrange("(p j) n -> p j n", j=PACK) for b in range(B)]
+        nc.sync.dma_start(k_pool[0][:], k_rows[0])
+        nc.sync.dma_start(vs_pool[0:1, :], vs[0:1, :])
+        nc.sync.dma_start(k_pool[1][:], k_rows[1])
+        nc.sync.dma_start(q_raw[0][:], q_rows[0])
+        nc.sync.dma_start(k_pool[2][:], k_rows[2])
+        nc.sync.dma_start(k_pool[3][:], k_rows[3])
+        nc.sync.dma_start(q_raw[1][:], q_rows[1])
+        nc.sync.dma_start(v_pool[0][:], vT[0:128, :])
+        nc.sync.dma_start(v_pool[1][:], vT[128:256, :])
+        nc.vector.memset(warm[:], 0.0)
+        nc.scalar.activation(warm[:], warm[:], ACT.Exp)
+        make_identity(nc, ident[:])
+
+        gather_v(0)
+        gather_v(1)
+        gather_k(0)
+        gather_k(2)
+        gather_k(1)
+        gather_vs()
+        gather_k_of(3, 0)
+        interleave_k(nc.scalar.copy, 0, 0)
+        interleave_q(nc.vector.tensor_copy, 0)
+        gather_k_of(3, 1)
+        interleave_k(nc.vector.tensor_copy, 2, 1)
+        quant_q(0)
+        interleave_k(nc.vector.tensor_copy, 2, 0)
+        quant_k(0)
+        scores(0,1)
+        interleave_q(nc.scalar.copy, 1)
+        turn_vs()
+        interleave_k(nc.vector.tensor_copy, 0, 1)
+        turn_v(0,0)
+        squash(0,1)
+        quant_q(1)
+        scores(0,0)
+        squash(0,0)
+        lowest(0,0)
+        quant_k(1)
+        scores(1,0)
+        expo(0,0)
+        pack_v(nc.scalar.copy, 0, 0)
+        lowest(0,1)
+        expo(0,1)
+        squash(1,0)
+        lowest(1,0)
+        turn_v(0,1)
+        expo(1,0)
+        scores(1,1)
+        squash(1,1)
+        lowest(1,1)
+        pack_v(nc.scalar.copy, 0, 1)
+        turn_w(0,0)
+        turn_v(1,0)
+        expo(1,1)
+        turn_w(0,1)
+        nc.vector.reciprocal(inv[:], totals[:])
+        turn_w(1,1)
+        weigh(0,0)
+        pack_v(nc.scalar.copy, 1, 0)
+        turn_v(1,1)
+        quant_w(0,0)
+        quant_v(0)
+        pack_v(nc.scalar.copy, 1, 1)
+        weigh(0,1)
+        quant_w(0,1)
+        turn_w(1,0)
+        weigh(1,1)
+        weigh(1,0)
+        product(0,1)
+        product(0,0)
+        quant_w(1,1)
+        finish(0, 0, True)
+        quant_v(1)
+        finish(0, 1, True)
+        product(1,1)
+        quant_w(1,0)
+        product(1,0)
+        finish(1, 0, True)
+        finish(1, 1, False)

@@ -16,6 +16,7 @@ BYTES = 4 * (B * D * NQ + D * T + DV * T + T + B * NQ * DV) + 2 * P * B * COLS
 
 F32 = mybir.dt.float32
 BF16 = mybir.dt.bfloat16
+I32 = mybir.dt.int32
 U32 = mybir.dt.uint32
 U16 = mybir.dt.uint16
 U8 = mybir.dt.uint8
@@ -23,18 +24,33 @@ FP8X4 = mybir.dt.float8_e4m3fn_x4
 ACT = mybir.ActivationFunctionType
 ALU = mybir.AluOpType
 
+K_CHUNKS = [
+    (0, 0, 1024, "scalar"),
+    (0, 1024, 2048, "vector"),
+    (1, 0, 1024, "scalar"),
+    (1, 1024, 1536, "vector"),
+    (1, 1536, 1792, "vector"),
+    (1, 1792, 2048, "vector"),
+]
+
 
 def tile_attend_gqa_cap_kernel(tc, qT, kT, vT, vs, offs, out):
     nc = tc.nc
     with ExitStack() as ctx:
         keep = ctx.enter_context(tc.tile_pool(name="keep", bufs=1))
-        work = ctx.enter_context(tc.tile_pool(name="work", bufs=4))
+        shared = ctx.enter_context(tc.tile_pool(name="shared", bufs=1))
         psum = ctx.enter_context(tc.psum_pool(name="psum", bufs=2))
+        units = [(b, m) for b in range(B) for m in range(QT)]
+
+        V_AT = [0, 4 * T]
+        Q_AT = [8 * T, 8 * T + 4 * PACK * NQ]
+        ROW = 4 * N
 
         offsets = keep.tile([P, B * COLS], U16, name="offsets")
-        k_pool = [keep.tile([P, T], F32, name=f"k_pool{t}") for t in range(PACK)]
-        v_pool = [keep.tile([P, T], F32, name=f"v_pool{h}") for h in range(VB)]
-        q_raw = [keep.tile([P, PACK, NQ], F32, name=f"q_raw{b}") for b in range(B)]
+        k_raw = [keep.tile([P, 2, c1 - c0], F32, name=f"k_raw{i}") for i, (u, c0, c1, e) in enumerate(K_CHUNKS)]
+        k_pairs = [keep.tile([P, T], U32, name=f"k_pairs{u}") for u in range(2)]
+        v_pool = [shared.tile([P, T], F32, name=f"v_pool{h}", offset=V_AT[h], align_bytes=64) for h in range(VB)]
+        q_raw = [shared.tile([P, PACK, NQ], F32, name=f"q_raw{b}", offset=Q_AT[b], align_bytes=64) for b in range(B)]
         vs_pool = keep.tile([P, T], F32, name="vs_pool")
         vs_row = keep.tile([P, B * N], F32, name="vs_row")
         vs_col = keep.tile([P, B, PACK], F32, name="vs_col")
@@ -45,58 +61,96 @@ def tile_attend_gqa_cap_kernel(tc, qT, kT, vT, vs, offs, out):
         q_packed = [keep.tile([P, NQ, PACK], BF16, name=f"q_packed{b}", align_bytes=64) for b in range(B)]
         q_codes = [keep.tile([P, NQ], U32, name=f"q_codes{b}", align_bytes=64) for b in range(B)]
         q_scales = [keep.tile([P, NQ], U8, name=f"q_scales{b}", align_bytes=64) for b in range(B)]
-        k_rows_of = keep.tile([P, PACK, B * N], F32, name="k_rows_of")
-        k_packed = [keep.tile([P, N, PACK], BF16, name=f"k_packed{b}", align_bytes=64) for b in range(B)]
-        k_codes = [keep.tile([P, N], U32, name=f"k_codes{b}", align_bytes=64) for b in range(B)]
+        k_words = keep.tile([P, 2, B * N], U32, name="k_words")
+        k_packed = [
+            keep.tile([P, N, 2], U32, name="k_packed0", align_bytes=64),
+            shared.tile([P, N, 2], U32, name="k_packed1", offset=Q_AT[0], align_bytes=64),
+        ]
+        k_codes = [
+            keep.tile([P, N], U32, name="k_codes0", align_bytes=64),
+            shared.tile([P, N], U32, name="k_codes1", offset=V_AT[0] + 2 * ROW, align_bytes=64),
+        ]
         k_scales = [keep.tile([P, N], U8, name=f"k_scales{b}", align_bytes=64) for b in range(B)]
-        v_rows = [keep.tile([P, B * N], F32, name=f"v_rows{h}") for h in range(VB)]
-        v_packed = [keep.tile([P, DV, PACK], BF16, name=f"v_packed{b}", align_bytes=64) for b in range(B)]
+        v_rows = [keep.tile([P, B * N], BF16, name=f"v_rows{h}", align_bytes=64) for h in range(VB)]
+        v_packed = [keep.tile([P, VB, P, 2], F32, name=f"v_packed{b}", align_bytes=64) for b in range(B)]
         v_codes = [keep.tile([P, DV], U32, name=f"v_codes{b}", align_bytes=64) for b in range(B)]
         v_scales = [keep.tile([P, DV], U8, name=f"v_scales{b}", align_bytes=64) for b in range(B)]
-        units = [(b, m) for b in range(B) for m in range(QT)]
-        w_codes = {u: keep.tile([P, P], U32, name=f"w_codes{u[0]}{u[1]}", align_bytes=64) for u in units}
-        w_scales = {u: keep.tile([P, P], U8, name=f"w_scales{u[0]}{u[1]}", align_bytes=64) for u in units}
-        w_packed = {u: keep.tile([P, P, PACK], BF16, name=f"w_packed{u[0]}{u[1]}", align_bytes=64) for u in units}
-        th = {u: keep.tile([P, N], F32, name=f"th{u[0]}{u[1]}") for u in units}
+        w_codes = [keep.tile([P, NQ], U32, name=f"w_codes{b}", align_bytes=64) for b in range(B)]
+        w_scales = [keep.tile([P, NQ], U8, name=f"w_scales{b}", align_bytes=64) for b in range(B)]
+        w_packed = [
+            shared.tile([P, NQ, PACK], BF16, name="w_packed0", offset=V_AT[1] + 2 * ROW, align_bytes=64),
+            keep.tile([P, NQ, PACK], BF16, name="w_packed1", align_bytes=64),
+        ]
+        p = {}
+        for m in range(QT):
+            p[0, m] = shared.tile([P, PACK, P], F32, name=f"p0{m}", offset=Q_AT[1] + m * ROW, align_bytes=64)
+            p[1, m] = keep.tile([P, PACK, P], F32, name=f"p1{m}")
+        neg = {
+            (b, m): shared.tile([P, PACK, P], F32, name=f"neg{b}{m}", offset=V_AT[b] + m * ROW, align_bytes=64)
+            for b, m in units
+        }
         low = {u: keep.tile([P, 1], F32, name=f"low{u[0]}{u[1]}") for u in units}
-        p = {u: keep.tile([P, PACK, P], F32, name=f"p{u[0]}{u[1]}") for u in units}
+        th = {u: keep.tile([P, PACK, P], F32, name=f"th{u[0]}{u[1]}") for u in units}
+        res = {u: keep.tile([P, DV], F32, name=f"res{u[0]}{u[1]}") for u in units}
         score, wt, vt, acc = {}, {}, {}, {}
-        over = {(0, 1): "v_pool0"}
 
         def quant(codes, scales, packed):
-            nc.vector.quantize_mx(out=codes.bitcast(FP8X4), scales=scales, in_=packed.rearrange("p n j -> p (n j)"))
+            nc.vector.quantize_mx(out=codes.bitcast(FP8X4), scales=scales, in_=packed)
 
-        def interleave_q(copy, b):
-            copy(q_packed[b][:], q_raw[b][:].rearrange("p j n -> p n j"))
+        def interleave_q(b):
+            nc.scalar.copy(
+                q_packed[b][:].rearrange("p (c i) j -> p c j i", i=4), q_raw[b][:].rearrange("p j (c i) -> p c j i", i=4)
+            )
 
         def quant_q(b):
-            quant(q_codes[b][:], q_scales[b][:], q_packed[b][:])
+            quant(q_codes[b][:], q_scales[b][:], q_packed[b][:].rearrange("p n j -> p (n j)"))
 
         def gather_vs():
             nc.vector.tensor_copy(vs_row[:], vs_pool[:].indirect(offsets[:]))
 
         def turn_vs():
             for b in range(B):
-                up = psum.tile([P, PACK, P], F32, name="turn", bufs=4)
+                up = psum.tile([P, PACK, P], F32, name="vturn", bufs=2)
                 for t in range(PACK):
                     nc.tensor.transpose(up[:, t, :], vs_row[:, b * N + t : (b + 1) * N : PACK], ident[:])
                 nc.scalar.copy(vs_col[:, b, :], up[:, :, 0])
 
-        def gather_k(t):
-            nc.vector.tensor_copy(k_rows_of[:, t, :], k_pool[t][:].indirect(offsets[:]))
+        def cast_k(i):
+            u, c0, c1, engine = K_CHUNKS[i]
+            dst = k_pairs[u][:, c0:c1].bitcast(BF16).rearrange("p (n j) -> p n j", j=2)
+            src = k_raw[i][:].rearrange("p j n -> p n j")
+            if engine == "scalar":
+                nc.scalar.activation(dst, src, ACT.Copy)
+            else:
+                nc.vector.tensor_copy(dst, src)
 
-        def gather_k_of(t, b):
-            nc.vector.tensor_copy(k_rows_of[:, t, b * N : (b + 1) * N], k_pool[t][:].indirect(offsets[:, b * COLS : (b + 1) * COLS]))
+        def gather_k(u):
+            nc.vector.tensor_copy(k_words[:, u, :], k_pairs[u][:].indirect(offsets[:]))
 
-        def interleave_k(copy, t, b):
-            copy(k_packed[b][:, :, t : t + 2], k_rows_of[:, t : t + 2, b * N : (b + 1) * N].rearrange("p j n -> p n j"))
+        def gather_k_of(u, b):
+            nc.vector.tensor_copy(
+                k_words[:, u, b * N : (b + 1) * N], k_pairs[u][:].indirect(offsets[:, b * COLS : (b + 1) * COLS])
+            )
 
-        def quant_k(b):
-            quant(k_codes[b][:], k_scales[b][:], k_packed[b][:])
+        def weave_k_vector(b, c0, c1):
+            nc.vector.tensor_copy(
+                k_packed[b][:].bitcast(I32)[:, c0:c1, :],
+                k_words[:].bitcast(I32)[:, :, b * N + c0 : b * N + c1].rearrange("p u n -> p n u"),
+            )
+
+        def weave_k_scalar(b):
+            nc.scalar.copy(k_packed[b][:], k_words[:, :, b * N : (b + 1) * N].rearrange("p u n -> p n u"))
+
+        def quant_k(b, c0, c1):
+            quant(
+                k_codes[b][:, c0:c1],
+                k_scales[b][:, c0:c1],
+                k_packed[b][:, c0:c1, :].rearrange("p n u -> p (n u)").bitcast(BF16),
+            )
 
         def scores(b, m):
             cols = slice(m * P, (m + 1) * P)
-            s = psum.tile([P, N], F32, name="score", bufs=2)
+            s = psum.tile([P, N], F32, name="acc", bufs=4)
             score[b, m] = s
             nc.tensor.matmul_mx(
                 out=s[:],
@@ -109,66 +163,62 @@ def tile_attend_gqa_cap_kernel(tc, qT, kT, vT, vs, offs, out):
             )
 
         def squash(*u):
-            nc.scalar.activation(th[u][:], score[u][:], ACT.Tanh, scale=1.0 / CAP)
+            nc.scalar.activation(
+                th[u][:], score[u][:].rearrange("q (s t) -> q t s", t=PACK), ACT.Tanh, scale=1.0 / CAP
+            )
 
         def lowest(*u):
-            if u in over:
-                neg = keep.tile([P, N], F32, name=f"neg{u[0]}{u[1]}", tag=over[u])
-            else:
-                neg = work.tile([P, N], F32, name="neg")
-            nc.vector.tensor_scalar(neg[:], th[u][:], -CAP, None, op0=ALU.mult, op1=ALU.min, accum_out=low[u][:])
+            nc.vector.tensor_scalar(
+                neg[u][:], th[u][:], -CAP, None, op0=ALU.mult, op1=ALU.min, accum_out=low[u][:]
+            )
 
         def expo(*u):
             i = units.index(u)
             nc.scalar.activation(
-                p[u][:].rearrange("q t s -> q s t"),
-                th[u][:].rearrange("q (s t) -> q s t", t=PACK),
-                ACT.Exp,
-                bias=low[u][:],
-                scale=CAP,
-                accum_out=totals[:, i : i + 1],
+                p[u][:], neg[u][:], ACT.Exp, bias=low[u][:], scale=-1.0, accum_out=totals[:, i : i + 1]
             )
 
         def turn_w(*u):
-            x = psum.tile([P, PACK, P], F32, name="turn", bufs=4)
+            x = psum.tile([P, PACK, P], F32, name="turn", bufs=2)
             wt[u] = x
             for t in range(PACK):
                 nc.tensor.transpose(x[:, t, :], p[u][:, t, :], ident[:])
 
-        def weigh(*u):
+        def weigh(b, m):
             nc.vector.tensor_tensor(
-                w_packed[u][:],
-                wt[u][:].rearrange("p t q -> p q t"),
-                vs_col[:, u[0], :].unsqueeze(1).to_broadcast([P, P, PACK]),
+                w_packed[b][:, m * P : (m + 1) * P, :],
+                wt[b, m][:].rearrange("p t q -> p q t"),
+                vs_col[:, b, :].unsqueeze(1).to_broadcast([P, P, PACK]),
                 ALU.mult,
             )
 
-        def quant_w(*u):
-            quant(w_codes[u][:], w_scales[u][:], w_packed[u][:])
+        def quant_w(b):
+            quant(w_codes[b][:], w_scales[b][:], w_packed[b][:].rearrange("p n j -> p (n j)"))
 
         def gather_v(h):
             nc.vector.tensor_copy(v_rows[h][:], v_pool[h][:].indirect(offsets[:]))
 
         def turn_v(h, b):
-            x = psum.tile([P, PACK, P], F32, name="turn", bufs=4)
-            vt[h, b] = x
-            for t in range(PACK):
-                nc.tensor.transpose(x[:, t, :], v_rows[h][:, b * N + t : (b + 1) * N : PACK], ident[:])
+            if h == 0:
+                vt[b] = psum.tile([P, VB, 2, P], F32, name="vturn", bufs=2)
+            words = v_rows[h][:].bitcast(F32)
+            for u in range(2):
+                nc.tensor.transpose(vt[b][:, h, u, :], words[:, b * N // 2 + u : (b + 1) * N // 2 : 2], ident[:])
 
-        def pack_v(copy, h, b):
-            copy(v_packed[b][:, h * P : (h + 1) * P, :], vt[h, b][:].rearrange("p t e -> p e t"))
+        def pack_v(b):
+            nc.scalar.copy(v_packed[b][:], vt[b][:].rearrange("p h u e -> p h e u"))
 
         def quant_v(b):
-            quant(v_codes[b][:], v_scales[b][:], v_packed[b][:])
+            quant(v_codes[b][:], v_scales[b][:], v_packed[b][:].rearrange("p h e u -> p (h e u)").bitcast(BF16))
 
-        def product(*u):
-            b = u[0]
-            y = psum.tile([P, DV], F32, name="y", bufs=2)
-            acc[u] = y
+        def product(b, m):
+            cols = slice(m * P, (m + 1) * P)
+            y = psum.tile([P, DV], F32, name="acc", bufs=4)
+            acc[b, m] = y
             nc.tensor.matmul_mx(
                 out=y[:],
-                lhsT=w_codes[u][:].bitcast(FP8X4),
-                lhsT_scale=w_scales[u][:],
+                lhsT=w_codes[b][:, cols].bitcast(FP8X4),
+                lhsT_scale=w_scales[b][:, cols],
                 rhs=v_codes[b][:].bitcast(FP8X4),
                 rhs_scale=v_scales[b][:],
                 start=True,
@@ -178,95 +228,88 @@ def tile_attend_gqa_cap_kernel(tc, qT, kT, vT, vs, offs, out):
         def finish(b, m, scalar):
             u = (b, m)
             i = units.index(u)
-            y = acc[u]
-            res = work.tile([P, DV], F32, name="res")
             if scalar:
-                nc.scalar.activation(res[:], y[:], ACT.Copy, scale=inv[:, i : i + 1])
+                nc.scalar.activation(res[u][:], acc[u][:], ACT.Copy, scale=inv[:, i : i + 1])
             else:
-                nc.vector.tensor_scalar(res[:], y[:], inv[:, i : i + 1], None, op0=ALU.mult)
-            nc.sync.dma_start(out[b, m * P : (m + 1) * P, :], res[:])
+                nc.vector.tensor_scalar(res[u][:], acc[u][:], inv[:, i : i + 1], None, op0=ALU.mult)
+            nc.sync.dma_start(out[b, m * P : (m + 1) * P, :], res[u][:])
 
         nc.gpsimd.memset(vs_pool[:, T // 2 : T], 0.0)
         nc.vector.memset(vs_pool[:, 0 : T // 2], 0.0)
+        k_rows = kT.rearrange("(p u j) n -> u p j n", u=2, j=2)
         nc.sync.dma_start(offsets[:], offs)
-        k_rows = kT.rearrange("(p j) n -> j p n", j=PACK)
-        q_rows = [qT[b].rearrange("(p j) n -> p j n", j=PACK) for b in range(B)]
-        nc.sync.dma_start(k_pool[0][:], k_rows[0])
-        nc.sync.dma_start(vs_pool[0:1, :], vs[0:1, :])
-        nc.sync.dma_start(k_pool[1][:], k_rows[1])
-        nc.sync.dma_start(q_raw[0][:], q_rows[0])
-        nc.sync.dma_start(k_pool[2][:], k_rows[2])
-        nc.sync.dma_start(k_pool[3][:], k_rows[3])
-        nc.sync.dma_start(q_raw[1][:], q_rows[1])
-        nc.sync.dma_start(v_pool[0][:], vT[0:128, :])
-        nc.sync.dma_start(v_pool[1][:], vT[128:256, :])
+        for i, (u, c0, c1, e) in enumerate(K_CHUNKS):
+            nc.sync.dma_start(k_raw[i][:], k_rows[u][:, :, c0:c1])
+            if i == 0:
+                nc.sync.dma_start(vs_pool[0:1, :], vs[0:1, :])
+        for b in range(B):
+            nc.sync.dma_start(q_raw[b][:], qT[b].rearrange("(p j) n -> p j n", j=PACK))
+            nc.sync.dma_start(v_pool[b][:], vT[b * P : (b + 1) * P, :])
         nc.vector.memset(warm[:], 0.0)
         nc.scalar.activation(warm[:], warm[:], ACT.Exp)
         make_identity(nc, ident[:])
 
-        gather_v(0)
-        gather_v(1)
-        gather_k(0)
-        gather_k(2)
-        gather_k(1)
+        cast_k(0)
         gather_vs()
-        gather_k_of(3, 0)
-        interleave_k(nc.scalar.copy, 0, 0)
-        interleave_q(nc.vector.tensor_copy, 0)
-        gather_k_of(3, 1)
-        interleave_k(nc.vector.tensor_copy, 2, 1)
-        quant_q(0)
-        interleave_k(nc.vector.tensor_copy, 2, 0)
-        quant_k(0)
-        scores(0,1)
-        interleave_q(nc.scalar.copy, 1)
+        cast_k(1)
+        gather_k(0)
         turn_vs()
-        interleave_k(nc.vector.tensor_copy, 0, 1)
-        turn_v(0,0)
-        squash(0,1)
+        for i in range(2, len(K_CHUNKS)):
+            cast_k(i)
+        gather_k_of(1, 0)
+        gather_k_of(1, 1)
+        interleave_q(0)
+        weave_k_vector(0, 0, N // 2)
+        weave_k_vector(0, N // 2, N)
+        quant_k(0, 0, N // 2)
+        quant_k(0, N // 2, N)
+        quant_q(0)
+        weave_k_scalar(1)
+        scores(0, 0)
+        scores(0, 1)
+        squash(0, 0)
+        squash(0, 1)
+        gather_v(0)
+        quant_k(1, 0, N)
+        interleave_q(1)
+        lowest(0, 0)
+        lowest(0, 1)
         quant_q(1)
-        scores(0,0)
-        squash(0,0)
-        lowest(0,0)
-        quant_k(1)
-        scores(1,0)
-        expo(0,0)
-        pack_v(nc.scalar.copy, 0, 0)
-        lowest(0,1)
-        expo(0,1)
-        squash(1,0)
-        lowest(1,0)
-        turn_v(0,1)
-        expo(1,0)
-        scores(1,1)
-        squash(1,1)
-        lowest(1,1)
-        pack_v(nc.scalar.copy, 0, 1)
-        turn_w(0,0)
-        turn_v(1,0)
-        expo(1,1)
-        turn_w(0,1)
-        nc.vector.reciprocal(inv[:], totals[:])
-        turn_w(1,1)
-        weigh(0,0)
-        pack_v(nc.scalar.copy, 1, 0)
-        turn_v(1,1)
-        quant_w(0,0)
+        turn_v(0, 0)
+        turn_v(0, 1)
+        scores(1, 0)
+        scores(1, 1)
+        expo(0, 0)
+        expo(0, 1)
+        squash(1, 0)
+        squash(1, 1)
+        gather_v(1)
+        turn_w(0, 0)
+        turn_w(0, 1)
+        turn_v(1, 0)
+        turn_v(1, 1)
+        weigh(0, 0)
+        lowest(1, 0)
+        lowest(1, 1)
+        weigh(0, 1)
+        pack_v(0)
+        expo(1, 0)
+        expo(1, 1)
+        pack_v(1)
+        turn_w(1, 0)
+        turn_w(1, 1)
         quant_v(0)
-        pack_v(nc.scalar.copy, 1, 1)
-        weigh(0,1)
-        quant_w(0,1)
-        turn_w(1,0)
-        weigh(1,1)
-        weigh(1,0)
-        product(0,1)
-        product(0,0)
-        quant_w(1,1)
-        finish(0, 0, True)
+        quant_w(0)
+        weigh(1, 0)
+        nc.vector.reciprocal(inv[:], totals[:])
+        weigh(1, 1)
+        product(0, 0)
+        product(0, 1)
         quant_v(1)
+        quant_w(1)
+        finish(0, 0, True)
         finish(0, 1, True)
-        product(1,1)
-        quant_w(1,0)
-        product(1,0)
+        product(1, 0)
+        product(1, 1)
         finish(1, 0, True)
         finish(1, 1, False)

@@ -39,12 +39,12 @@ def tile_attend_gqa_cap_kernel(tc, qT, kT, vT, vs, offs, out):
     with ExitStack() as ctx:
         keep = ctx.enter_context(tc.tile_pool(name="keep", bufs=1))
         shared = ctx.enter_context(tc.tile_pool(name="shared", bufs=1))
-        psum = ctx.enter_context(tc.psum_pool(name="psum", bufs=2))
+        psum = ctx.enter_context(tc.psum_pool(name="psum", bufs=1))
         units = [(b, m) for b in range(B) for m in range(QT)]
 
-        V_AT = [0, 4 * T]
-        Q_AT = [8 * T, 8 * T + 4 * PACK * NQ]
         ROW = 4 * N
+        V_AT = [0, 4 * ROW]
+        Q_AT = [8 * ROW, 11 * ROW]
 
         offsets = keep.tile([P, B * COLS], U16, name="offsets")
         k_raw = [keep.tile([P, 2, c1 - c0], F32, name=f"k_raw{i}") for i, (u, c0, c1, e) in enumerate(K_CHUNKS)]
@@ -57,7 +57,7 @@ def tile_attend_gqa_cap_kernel(tc, qT, kT, vT, vs, offs, out):
         ident = keep.tile([P, P], F32, name="ident")
         warm = keep.tile([P, 1], F32, name="warm")
         totals = keep.tile([P, B * QT], F32, name="totals")
-        inv = keep.tile([P, B * QT], F32, name="inv")
+        inv = shared.tile([P, B * QT], F32, name="inv", offset=V_AT[1] + 3 * ROW, align_bytes=64)
         q_packed = [keep.tile([P, NQ, PACK], BF16, name=f"q_packed{b}", align_bytes=64) for b in range(B)]
         q_codes = [keep.tile([P, NQ], U32, name=f"q_codes{b}", align_bytes=64) for b in range(B)]
         q_scales = [keep.tile([P, NQ], U8, name=f"q_scales{b}", align_bytes=64) for b in range(B)]
@@ -68,29 +68,32 @@ def tile_attend_gqa_cap_kernel(tc, qT, kT, vT, vs, offs, out):
         ]
         k_codes = [
             keep.tile([P, N], U32, name="k_codes0", align_bytes=64),
-            shared.tile([P, N], U32, name="k_codes1", offset=V_AT[0] + 2 * ROW, align_bytes=64),
+            shared.tile([P, N], U32, name="k_codes1", offset=Q_AT[1] + ROW // 2, align_bytes=64),
         ]
         k_scales = [keep.tile([P, N], U8, name=f"k_scales{b}", align_bytes=64) for b in range(B)]
         v_rows = [keep.tile([P, B * N], BF16, name=f"v_rows{h}", align_bytes=64) for h in range(VB)]
-        v_packed = [keep.tile([P, VB, P, 2], F32, name=f"v_packed{b}", align_bytes=64) for b in range(B)]
+        v_packed = [
+            shared.tile([P, VB, P, 2], F32, name=f"v_packed{b}", offset=V_AT[0] + (3 - b) * ROW, align_bytes=64)
+            for b in range(B)
+        ]
         v_codes = [keep.tile([P, DV], U32, name=f"v_codes{b}", align_bytes=64) for b in range(B)]
         v_scales = [keep.tile([P, DV], U8, name=f"v_scales{b}", align_bytes=64) for b in range(B)]
         w_codes = [keep.tile([P, NQ], U32, name=f"w_codes{b}", align_bytes=64) for b in range(B)]
         w_scales = [keep.tile([P, NQ], U8, name=f"w_scales{b}", align_bytes=64) for b in range(B)]
         w_packed = [
-            shared.tile([P, NQ, PACK], BF16, name="w_packed0", offset=V_AT[1] + 2 * ROW, align_bytes=64),
-            keep.tile([P, NQ, PACK], BF16, name="w_packed1", align_bytes=64),
+            shared.tile([P, NQ, PACK], BF16, name=f"w_packed{b}", offset=V_AT[1] + b * ROW, align_bytes=64)
+            for b in range(B)
         ]
-        p = {}
+        th = {}
         for m in range(QT):
-            p[0, m] = shared.tile([P, PACK, P], F32, name=f"p0{m}", offset=Q_AT[1] + m * ROW, align_bytes=64)
-            p[1, m] = keep.tile([P, PACK, P], F32, name=f"p1{m}")
+            th[0, m] = shared.tile([P, PACK, P], F32, name=f"th0{m}", offset=Q_AT[1] - ROW // 2 + 2 * m * ROW, align_bytes=64)
+            th[1, m] = keep.tile([P, PACK, P], F32, name=f"th1{m}")
         neg = {
-            (b, m): shared.tile([P, PACK, P], F32, name=f"neg{b}{m}", offset=V_AT[b] + m * ROW, align_bytes=64)
+            (b, m): shared.tile([P, PACK, P], F32, name=f"neg{b}{m}", offset=V_AT[0] + (2 * b + m) * ROW, align_bytes=64)
             for b, m in units
         }
         low = {u: keep.tile([P, 1], F32, name=f"low{u[0]}{u[1]}") for u in units}
-        th = {u: keep.tile([P, PACK, P], F32, name=f"th{u[0]}{u[1]}") for u in units}
+        p = {u: keep.tile([P, PACK, P], F32, name=f"p{u[0]}{u[1]}") for u in units}
         res = {u: keep.tile([P, DV], F32, name=f"res{u[0]}{u[1]}") for u in units}
         score, wt, vt, acc = {}, {}, {}, {}
 
@@ -110,7 +113,7 @@ def tile_attend_gqa_cap_kernel(tc, qT, kT, vT, vs, offs, out):
 
         def turn_vs():
             for b in range(B):
-                up = psum.tile([P, PACK, P], F32, name="vturn", bufs=2)
+                up = psum.tile([P, PACK, P], F32, name=f"bank{4 + b}")
                 for t in range(PACK):
                     nc.tensor.transpose(up[:, t, :], vs_row[:, b * N + t : (b + 1) * N : PACK], ident[:])
                 nc.scalar.copy(vs_col[:, b, :], up[:, :, 0])
@@ -150,7 +153,7 @@ def tile_attend_gqa_cap_kernel(tc, qT, kT, vT, vs, offs, out):
 
         def scores(b, m):
             cols = slice(m * P, (m + 1) * P)
-            s = psum.tile([P, N], F32, name="acc", bufs=4)
+            s = psum.tile([P, N], F32, name=f"bank{2 * b + m}")
             score[b, m] = s
             nc.tensor.matmul_mx(
                 out=s[:],
@@ -179,7 +182,7 @@ def tile_attend_gqa_cap_kernel(tc, qT, kT, vT, vs, offs, out):
             )
 
         def turn_w(*u):
-            x = psum.tile([P, PACK, P], F32, name="turn", bufs=2)
+            x = psum.tile([P, PACK, P], F32, name=f"bank{6 - 6 * u[0] + u[1]}")
             wt[u] = x
             for t in range(PACK):
                 nc.tensor.transpose(x[:, t, :], p[u][:, t, :], ident[:])
@@ -192,28 +195,32 @@ def tile_attend_gqa_cap_kernel(tc, qT, kT, vT, vs, offs, out):
                 ALU.mult,
             )
 
-        def quant_w(b):
-            quant(w_codes[b][:], w_scales[b][:], w_packed[b][:].rearrange("p n j -> p (n j)"))
+        def quant_w(b, c0, c1):
+            quant(w_codes[b][:, c0:c1], w_scales[b][:, c0:c1], w_packed[b][:, c0:c1, :].rearrange("p n j -> p (n j)"))
 
         def gather_v(h):
             nc.vector.tensor_copy(v_rows[h][:], v_pool[h][:].indirect(offsets[:]))
 
-        def turn_v(h, b):
-            if h == 0:
-                vt[b] = psum.tile([P, VB, 2, P], F32, name="vturn", bufs=2)
+        def gather_v_of(h, b):
+            nc.vector.tensor_copy(
+                v_rows[h][:, b * N : (b + 1) * N], v_pool[h][:].indirect(offsets[:, b * COLS : (b + 1) * COLS])
+            )
+
+        def turn_v(h, b, bank):
+            vt[h, b] = psum.tile([P, 2, P], F32, name=f"bank{bank}")
             words = v_rows[h][:].bitcast(F32)
             for u in range(2):
-                nc.tensor.transpose(vt[b][:, h, u, :], words[:, b * N // 2 + u : (b + 1) * N // 2 : 2], ident[:])
+                nc.tensor.transpose(vt[h, b][:, u, :], words[:, b * N // 2 + u : (b + 1) * N // 2 : 2], ident[:])
 
-        def pack_v(b):
-            nc.scalar.copy(v_packed[b][:], vt[b][:].rearrange("p h u e -> p h e u"))
+        def pack_v(h, b):
+            nc.scalar.copy(v_packed[b][:, h, :, :], vt[h, b][:].rearrange("p u e -> p e u"))
 
         def quant_v(b):
             quant(v_codes[b][:], v_scales[b][:], v_packed[b][:].rearrange("p h e u -> p (h e u)").bitcast(BF16))
 
         def product(b, m):
             cols = slice(m * P, (m + 1) * P)
-            y = psum.tile([P, DV], F32, name="acc", bufs=4)
+            y = psum.tile([P, DV], F32, name=f"bank{2 + 4 * b + m}")
             acc[b, m] = y
             nc.tensor.matmul_mx(
                 out=y[:],
@@ -244,7 +251,8 @@ def tile_attend_gqa_cap_kernel(tc, qT, kT, vT, vs, offs, out):
                 nc.sync.dma_start(vs_pool[0:1, :], vs[0:1, :])
         for b in range(B):
             nc.sync.dma_start(q_raw[b][:], qT[b].rearrange("(p j) n -> p j n", j=PACK))
-            nc.sync.dma_start(v_pool[b][:], vT[b * P : (b + 1) * P, :])
+        for h in range(VB):
+            nc.sync.dma_start(v_pool[h][:], vT[h * P : (h + 1) * P, :])
         nc.vector.memset(warm[:], 0.0)
         nc.scalar.activation(warm[:], warm[:], ACT.Exp)
         make_identity(nc, ident[:])
@@ -259,54 +267,45 @@ def tile_attend_gqa_cap_kernel(tc, qT, kT, vT, vs, offs, out):
         gather_k_of(1, 0)
         gather_k_of(1, 1)
         interleave_q(0)
+        interleave_q(1)
         weave_k_vector(0, 0, N // 2)
         weave_k_vector(0, N // 2, N)
         quant_k(0, 0, N // 2)
         quant_k(0, N // 2, N)
         quant_q(0)
-        weave_k_scalar(1)
-        scores(0, 0)
-        scores(0, 1)
-        squash(0, 0)
-        squash(0, 1)
-        gather_v(0)
-        quant_k(1, 0, N)
-        interleave_q(1)
-        lowest(0, 0)
-        lowest(0, 1)
+        weave_k_vector(1, 0, N)
         quant_q(1)
-        turn_v(0, 0)
-        turn_v(0, 1)
-        scores(1, 0)
-        scores(1, 1)
-        expo(0, 0)
-        expo(0, 1)
-        squash(1, 0)
-        squash(1, 1)
-        gather_v(1)
-        turn_w(0, 0)
-        turn_w(0, 1)
-        turn_v(1, 0)
-        turn_v(1, 1)
+        quant_k(1, 0, N)
+        for u in units:
+            scores(*u)
+            squash(*u)
+        gather_v(0)
+        turn_v(0, 0, 4)
+        turn_v(0, 1, 5)
+        for u in units:
+            lowest(*u)
+            expo(*u)
+            turn_w(*u)
+        pack_v(0, 0)
+        pack_v(0, 1)
+        gather_v_of(1, 0)
+        gather_v_of(1, 1)
+        turn_v(1, 0, 2)
+        turn_v(1, 1, 3)
+        pack_v(1, 0)
+        pack_v(1, 1)
         weigh(0, 0)
-        lowest(1, 0)
-        lowest(1, 1)
         weigh(0, 1)
-        pack_v(0)
-        expo(1, 0)
-        expo(1, 1)
-        pack_v(1)
-        turn_w(1, 0)
-        turn_w(1, 1)
-        quant_v(0)
-        quant_w(0)
         weigh(1, 0)
-        nc.vector.reciprocal(inv[:], totals[:])
+        quant_w(0, 0, NQ)
+        quant_v(0)
         weigh(1, 1)
+        nc.vector.reciprocal(inv[:], totals[:])
         product(0, 0)
         product(0, 1)
         quant_v(1)
-        quant_w(1)
+        quant_w(1, 0, P)
+        quant_w(1, P, NQ)
         finish(0, 0, True)
         finish(0, 1, True)
         product(1, 0)

@@ -25,12 +25,12 @@ ACT = mybir.ActivationFunctionType
 ALU = mybir.AluOpType
 
 K_CHUNKS = [
-    (0, 0, 1024, "scalar"),
-    (0, 1024, 2048, "vector"),
-    (1, 0, 1024, "scalar"),
-    (1, 1024, 1536, "vector"),
-    (1, 1536, 1792, "vector"),
-    (1, 1792, 2048, "vector"),
+    (0, 0, 1024, 1024),
+    (0, 1024, 2048, 384),
+    (1, 0, 1024, 1024),
+    (1, 1024, 1536, 0),
+    (1, 1536, 1792, 0),
+    (1, 1792, 2048, 0),
 ]
 
 
@@ -45,15 +45,21 @@ def tile_attend_gqa_cap_kernel(tc, qT, kT, vT, vs, offs, out):
         ROW = 4 * N
         V_AT = [0, 4 * ROW]
         Q_AT = [8 * ROW, 11 * ROW]
+        K_AT = 16 * ROW
 
         offsets = keep.tile([P, B * COLS], U16, name="offsets")
-        k_raw = [keep.tile([P, 2, c1 - c0], F32, name=f"k_raw{i}") for i, (u, c0, c1, e) in enumerate(K_CHUNKS)]
+        k_raw = [
+            shared.tile([P, 2, c1 - c0], F32, name=f"k_raw{i}", offset=K_AT, align_bytes=64)
+            if i == 2
+            else keep.tile([P, 2, c1 - c0], F32, name=f"k_raw{i}")
+            for i, (u, c0, c1, e) in enumerate(K_CHUNKS)
+        ]
         k_pairs = [keep.tile([P, T], U32, name=f"k_pairs{u}") for u in range(2)]
         v_pool = [shared.tile([P, T], F32, name=f"v_pool{h}", offset=V_AT[h], align_bytes=64) for h in range(VB)]
         q_raw = [shared.tile([P, PACK, NQ], F32, name=f"q_raw{b}", offset=Q_AT[b], align_bytes=64) for b in range(B)]
         vs_pool = keep.tile([P, T], F32, name="vs_pool")
         vs_row = keep.tile([P, B * N], F32, name="vs_row")
-        vs_col = keep.tile([P, B, PACK], F32, name="vs_col")
+        vs_col = shared.tile([P, B, PACK], F32, name="vs_col", offset=K_AT, align_bytes=64)
         ident = keep.tile([P, P], F32, name="ident")
         warm = keep.tile([P, 1], F32, name="warm")
         totals = keep.tile([P, B * QT], F32, name="totals")
@@ -62,15 +68,18 @@ def tile_attend_gqa_cap_kernel(tc, qT, kT, vT, vs, offs, out):
         q_codes = [keep.tile([P, NQ], U32, name=f"q_codes{b}", align_bytes=64) for b in range(B)]
         q_scales = [keep.tile([P, NQ], U8, name=f"q_scales{b}", align_bytes=64) for b in range(B)]
         k_words = keep.tile([P, 2, B * N], U32, name="k_words")
-        k_packed = [
-            keep.tile([P, N, 2], U32, name="k_packed0", align_bytes=64),
-            shared.tile([P, N, 2], U32, name="k_packed1", offset=Q_AT[0], align_bytes=64),
+        H = N // 2
+        k_packed = {
+            (0, 0): keep.tile([P, H, 2], U32, name="k_packed00", align_bytes=64),
+            (0, 1): keep.tile([P, H, 2], U32, name="k_packed01", align_bytes=64),
+            (1, 0): shared.tile([P, H, 2], U32, name="k_packed10", offset=Q_AT[0], align_bytes=64),
+            (1, 1): shared.tile([P, H, 2], U32, name="k_packed11", offset=Q_AT[1] - ROW + 64, align_bytes=64),
+        }
+        k_codes = [keep.tile([P, N], U32, name=f"k_codes{b}", align_bytes=64) for b in range(B)]
+        k_scales = [
+            keep.tile([P, N], U8, name="k_scales0", align_bytes=64),
+            shared.tile([P, N], U8, name="k_scales1", offset=Q_AT[1] + 64, align_bytes=64),
         ]
-        k_codes = [
-            keep.tile([P, N], U32, name="k_codes0", align_bytes=64),
-            shared.tile([P, N], U32, name="k_codes1", offset=Q_AT[1] + ROW // 2, align_bytes=64),
-        ]
-        k_scales = [keep.tile([P, N], U8, name=f"k_scales{b}", align_bytes=64) for b in range(B)]
         v_rows = [keep.tile([P, B * N], BF16, name=f"v_rows{h}", align_bytes=64) for h in range(VB)]
         v_packed = [
             shared.tile([P, VB, P, 2], F32, name=f"v_packed{b}", offset=V_AT[0] + (3 - b) * ROW, align_bytes=64)
@@ -84,14 +93,16 @@ def tile_attend_gqa_cap_kernel(tc, qT, kT, vT, vs, offs, out):
             shared.tile([P, NQ, PACK], BF16, name=f"w_packed{b}", offset=V_AT[1] + b * ROW, align_bytes=64)
             for b in range(B)
         ]
-        th = {}
-        for m in range(QT):
-            th[0, m] = shared.tile([P, PACK, P], F32, name=f"th0{m}", offset=Q_AT[1] - ROW // 2 + 2 * m * ROW, align_bytes=64)
-            th[1, m] = keep.tile([P, PACK, P], F32, name=f"th1{m}")
+        th_of = [
+            shared.tile([P, QT, N], F32, name="th0", offset=Q_AT[1] + 2 * ROW - 64, align_bytes=64),
+            keep.tile([P, QT, N], F32, name="th1"),
+        ]
+        th = {(b, m): th_of[b][:, m, :] for b, m in units}
         neg = {
-            (b, m): shared.tile([P, PACK, P], F32, name=f"neg{b}{m}", offset=V_AT[0] + (2 * b + m) * ROW, align_bytes=64)
+            (b, m): shared.tile([P, N], F32, name=f"neg{b}{m}", offset=V_AT[0] + (2 * b + m) * ROW, align_bytes=64)
             for b, m in units
         }
+        w_planes = [keep.tile([P, PACK, P], BF16, name=f"w_planes{m}") for m in range(QT)]
         low = {u: keep.tile([P, 1], F32, name=f"low{u[0]}{u[1]}") for u in units}
         p = {u: keep.tile([P, PACK, P], F32, name=f"p{u[0]}{u[1]}") for u in units}
         res = {u: keep.tile([P, DV], F32, name=f"res{u[0]}{u[1]}") for u in units}
@@ -119,13 +130,14 @@ def tile_attend_gqa_cap_kernel(tc, qT, kT, vT, vs, offs, out):
                 nc.scalar.copy(vs_col[:, b, :], up[:, :, 0])
 
         def cast_k(i):
-            u, c0, c1, engine = K_CHUNKS[i]
-            dst = k_pairs[u][:, c0:c1].bitcast(BF16).rearrange("p (n j) -> p n j", j=2)
-            src = k_raw[i][:].rearrange("p j n -> p n j")
-            if engine == "scalar":
-                nc.scalar.activation(dst, src, ACT.Copy)
-            else:
-                nc.vector.tensor_copy(dst, src)
+            u, c0, c1, share = K_CHUNKS[i]
+            for copy, a, z in ((cast_scalar, 0, share), (nc.vector.tensor_copy, share, c1 - c0)):
+                if a < z:
+                    dst = k_pairs[u][:, c0 + a : c0 + z].bitcast(BF16).rearrange("p (n j) -> p n j", j=2)
+                    copy(dst, k_raw[i][:, :, a:z].rearrange("p j n -> p n j"))
+
+        def cast_scalar(dst, src):
+            nc.scalar.activation(dst, src, ACT.Copy)
 
         def gather_k(u):
             nc.vector.tensor_copy(k_words[:, u, :], k_pairs[u][:].indirect(offsets[:]))
@@ -135,21 +147,13 @@ def tile_attend_gqa_cap_kernel(tc, qT, kT, vT, vs, offs, out):
                 k_words[:, u, b * N : (b + 1) * N], k_pairs[u][:].indirect(offsets[:, b * COLS : (b + 1) * COLS])
             )
 
-        def weave_k_vector(b, c0, c1):
-            nc.vector.tensor_copy(
-                k_packed[b][:].bitcast(I32)[:, c0:c1, :],
-                k_words[:].bitcast(I32)[:, :, b * N + c0 : b * N + c1].rearrange("p u n -> p n u"),
-            )
+        def weave_k(copy, word, b, c):
+            cols = slice(b * N + c * H, b * N + (c + 1) * H)
+            copy(k_packed[b, c][:].bitcast(word), k_words[:].bitcast(word)[:, :, cols].rearrange("p u n -> p n u"))
 
-        def weave_k_scalar(b):
-            nc.scalar.copy(k_packed[b][:], k_words[:, :, b * N : (b + 1) * N].rearrange("p u n -> p n u"))
-
-        def quant_k(b, c0, c1):
-            quant(
-                k_codes[b][:, c0:c1],
-                k_scales[b][:, c0:c1],
-                k_packed[b][:, c0:c1, :].rearrange("p n u -> p (n u)").bitcast(BF16),
-            )
+        def quant_k(b, c):
+            cols = slice(c * H, (c + 1) * H)
+            quant(k_codes[b][:, cols], k_scales[b][:, cols], k_packed[b, c][:].rearrange("p n u -> p (n u)").bitcast(BF16))
 
         def scores(b, m):
             cols = slice(m * P, (m + 1) * P)
@@ -166,19 +170,22 @@ def tile_attend_gqa_cap_kernel(tc, qT, kT, vT, vs, offs, out):
             )
 
         def squash(*u):
-            nc.scalar.activation(
-                th[u][:], score[u][:].rearrange("q (s t) -> q t s", t=PACK), ACT.Tanh, scale=1.0 / CAP
-            )
+            nc.scalar.activation(th[u], score[u][:], ACT.Tanh, scale=1.0 / CAP)
 
         def lowest(*u):
             nc.vector.tensor_scalar(
-                neg[u][:], th[u][:], -CAP, None, op0=ALU.mult, op1=ALU.min, accum_out=low[u][:]
+                neg[u][:], th[u], -CAP, None, op0=ALU.mult, op1=ALU.min, accum_out=low[u][:]
             )
 
         def expo(*u):
             i = units.index(u)
             nc.scalar.activation(
-                p[u][:], neg[u][:], ACT.Exp, bias=low[u][:], scale=-1.0, accum_out=totals[:, i : i + 1]
+                p[u][:].rearrange("q t s -> q s t"),
+                neg[u][:].rearrange("q (s t) -> q s t", t=PACK),
+                ACT.Exp,
+                bias=low[u][:],
+                scale=-1.0,
+                accum_out=totals[:, i : i + 1],
             )
 
         def turn_w(*u):
@@ -194,6 +201,11 @@ def tile_attend_gqa_cap_kernel(tc, qT, kT, vT, vs, offs, out):
                 vs_col[:, b, :].unsqueeze(1).to_broadcast([P, P, PACK]),
                 ALU.mult,
             )
+
+        def weigh_scalar(b, m):
+            for t in range(PACK):
+                nc.scalar.activation(w_planes[m][:, t, :], wt[b, m][:, t, :], ACT.Copy, scale=vs_col[:, b, t : t + 1])
+            nc.scalar.copy(w_packed[b][:, m * P : (m + 1) * P, :], w_planes[m][:].rearrange("p t q -> p q t"))
 
         def quant_w(b, c0, c1):
             quant(w_codes[b][:, c0:c1], w_scales[b][:, c0:c1], w_packed[b][:, c0:c1, :].rearrange("p n j -> p (n j)"))
@@ -261,21 +273,23 @@ def tile_attend_gqa_cap_kernel(tc, qT, kT, vT, vs, offs, out):
         gather_vs()
         cast_k(1)
         gather_k(0)
-        turn_vs()
         for i in range(2, len(K_CHUNKS)):
             cast_k(i)
+        turn_vs()
         gather_k_of(1, 0)
         gather_k_of(1, 1)
         interleave_q(0)
         interleave_q(1)
-        weave_k_vector(0, 0, N // 2)
-        weave_k_vector(0, N // 2, N)
-        quant_k(0, 0, N // 2)
-        quant_k(0, N // 2, N)
+        weave_k(nc.vector.tensor_copy, I32, 0, 0)
+        weave_k(nc.vector.tensor_copy, I32, 0, 1)
+        quant_k(0, 0)
+        quant_k(0, 1)
         quant_q(0)
-        weave_k_vector(1, 0, N)
+        weave_k(nc.scalar.copy, U32, 1, 1)
+        weave_k(nc.vector.tensor_copy, I32, 1, 0)
         quant_q(1)
-        quant_k(1, 0, N)
+        quant_k(1, 0)
+        quant_k(1, 1)
         for u in units:
             scores(*u)
             squash(*u)
@@ -286,6 +300,7 @@ def tile_attend_gqa_cap_kernel(tc, qT, kT, vT, vs, offs, out):
             lowest(*u)
             expo(*u)
             turn_w(*u)
+        weigh_scalar(0, 0)
         pack_v(0, 0)
         pack_v(0, 1)
         gather_v_of(1, 0)
@@ -294,7 +309,6 @@ def tile_attend_gqa_cap_kernel(tc, qT, kT, vT, vs, offs, out):
         turn_v(1, 1, 3)
         pack_v(1, 0)
         pack_v(1, 1)
-        weigh(0, 0)
         weigh(0, 1)
         weigh(1, 0)
         quant_w(0, 0, NQ)

@@ -82,8 +82,8 @@ def tile_attend_gqa_cap_kernel(tc, qT, kT, vT, vs, offs, out):
         ]
         v_rows = [keep.tile([P, B * N], BF16, name=f"v_rows{h}", align_bytes=64) for h in range(VB)]
         v_packed = [
-            shared.tile([P, VB, P, 2], F32, name=f"v_packed{b}", offset=V_AT[0] + (3 - b) * ROW, align_bytes=64)
-            for b in range(B)
+            keep.tile([P, VB, P, 2], F32, name="v_packed0", align_bytes=64),
+            shared.tile([P, VB, P, 2], F32, name="v_packed1", offset=V_AT[0] + 3 * ROW, align_bytes=64),
         ]
         v_codes = [keep.tile([P, DV], U32, name=f"v_codes{b}", align_bytes=64) for b in range(B)]
         v_scales = [keep.tile([P, DV], U8, name=f"v_scales{b}", align_bytes=64) for b in range(B)]
@@ -102,7 +102,7 @@ def tile_attend_gqa_cap_kernel(tc, qT, kT, vT, vs, offs, out):
             (b, m): shared.tile([P, N], F32, name=f"neg{b}{m}", offset=V_AT[0] + (2 * b + m) * ROW, align_bytes=64)
             for b, m in units
         }
-        w_planes = [keep.tile([P, PACK, P], BF16, name=f"w_planes{m}") for m in range(QT)]
+        w_planes = keep.tile([P, PACK, P], BF16, name="w_planes")
         low = {u: keep.tile([P, 1], F32, name=f"low{u[0]}{u[1]}") for u in units}
         p = {u: keep.tile([P, PACK, P], F32, name=f"p{u[0]}{u[1]}") for u in units}
         res = {u: keep.tile([P, DV], F32, name=f"res{u[0]}{u[1]}") for u in units}
@@ -170,7 +170,12 @@ def tile_attend_gqa_cap_kernel(tc, qT, kT, vT, vs, offs, out):
             )
 
         def squash(*u):
-            nc.scalar.activation(th[u], score[u][:], ACT.Tanh, scale=1.0 / CAP)
+            nc.scalar.activation(
+                th[u].rearrange("q (t s) -> q t s", t=PACK),
+                score[u][:].rearrange("q (s t) -> q t s", t=PACK),
+                ACT.Tanh,
+                scale=1.0 / CAP,
+            )
 
         def lowest(*u):
             nc.vector.tensor_scalar(
@@ -180,8 +185,8 @@ def tile_attend_gqa_cap_kernel(tc, qT, kT, vT, vs, offs, out):
         def expo(*u):
             i = units.index(u)
             nc.scalar.activation(
-                p[u][:].rearrange("q t s -> q s t"),
-                neg[u][:].rearrange("q (s t) -> q s t", t=PACK),
+                p[u][:].rearrange("q t s -> q (t s)"),
+                neg[u][:],
                 ACT.Exp,
                 bias=low[u][:],
                 scale=-1.0,
@@ -204,8 +209,8 @@ def tile_attend_gqa_cap_kernel(tc, qT, kT, vT, vs, offs, out):
 
         def weigh_scalar(b, m):
             for t in range(PACK):
-                nc.scalar.activation(w_planes[m][:, t, :], wt[b, m][:, t, :], ACT.Copy, scale=vs_col[:, b, t : t + 1])
-            nc.scalar.copy(w_packed[b][:, m * P : (m + 1) * P, :], w_planes[m][:].rearrange("p t q -> p q t"))
+                nc.scalar.activation(w_planes[:, t, :], wt[b, m][:, t, :], ACT.Copy, scale=vs_col[:, b, t : t + 1])
+            nc.scalar.copy(w_packed[b][:, m * P : (m + 1) * P, :], w_planes[:].rearrange("p t q -> p q t"))
 
         def quant_w(b, c0, c1):
             quant(w_codes[b][:, c0:c1], w_scales[b][:, c0:c1], w_packed[b][:, c0:c1, :].rearrange("p n j -> p (n j)"))
@@ -256,10 +261,10 @@ def tile_attend_gqa_cap_kernel(tc, qT, kT, vT, vs, offs, out):
         nc.gpsimd.memset(vs_pool[:, T // 2 : T], 0.0)
         nc.vector.memset(vs_pool[:, 0 : T // 2], 0.0)
         k_rows = kT.rearrange("(p u j) n -> u p j n", u=2, j=2)
-        nc.sync.dma_start(offsets[:], offs)
         for i, (u, c0, c1, e) in enumerate(K_CHUNKS):
             nc.sync.dma_start(k_raw[i][:], k_rows[u][:, :, c0:c1])
             if i == 0:
+                nc.sync.dma_start(offsets[:], offs)
                 nc.sync.dma_start(vs_pool[0:1, :], vs[0:1, :])
         for b in range(B):
             nc.sync.dma_start(q_raw[b][:], qT[b].rearrange("(p j) n -> p j n", j=PACK))
@@ -293,18 +298,18 @@ def tile_attend_gqa_cap_kernel(tc, qT, kT, vT, vs, offs, out):
         for u in units:
             scores(*u)
             squash(*u)
-        gather_v(0)
+        gather_v_of(0, 0)
+        gather_v_of(0, 1)
         turn_v(0, 0, 4)
         turn_v(0, 1, 5)
+        pack_v(0, 0)
         for u in units:
             lowest(*u)
             expo(*u)
             turn_w(*u)
         weigh_scalar(0, 0)
-        pack_v(0, 0)
         pack_v(0, 1)
-        gather_v_of(1, 0)
-        gather_v_of(1, 1)
+        gather_v(1)
         turn_v(1, 0, 2)
         turn_v(1, 1, 3)
         pack_v(1, 0)

@@ -10,6 +10,7 @@ CAP = 2.0
 QT = NQ // P
 VB = DV // P
 COLS = N // 16
+HALF = N // 2
 
 FLOPS = 2 * B * NQ * N * (D + DV)
 BYTES = 4 * (B * D * NQ + D * T + DV * T + T + B * NQ * DV) + 2 * P * B * COLS
@@ -24,14 +25,28 @@ FP8X4 = mybir.dt.float8_e4m3fn_x4
 ACT = mybir.ActivationFunctionType
 ALU = mybir.AluOpType
 
-K_CHUNKS = [
-    (0, 0, 1024, 1024),
-    (0, 1024, 2048, 384),
-    (1, 0, 1024, 1024),
-    (1, 1024, 1536, 0),
-    (1, 1536, 1792, 0),
-    (1, 1792, 2048, 0),
+K_LOADS = [
+    (0, 0, T // 2, T // 2),
+    (0, T // 2, T, 3 * T // 16),
+    (1, 0, T // 2, T // 2),
+    (1, T // 2, 3 * T // 4, 0),
+    (1, 3 * T // 4, 7 * T // 8, 0),
+    (1, 7 * T // 8, T, 0),
 ]
+LAST_OF_WINDOW_0 = 1
+LAST_SCALAR_CAST = 2
+
+ROW = 4 * N
+EDGE = 64
+V_AT = [0, 4 * ROW]
+Q_AT = [8 * ROW, 11 * ROW]
+K_AT = 16 * ROW
+
+SCORE_BANK = {(0, 0): 0, (0, 1): 1, (1, 0): 2, (1, 1): 3}
+VS_BANK = [4, 5]
+V_BANK = {(0, 0): 4, (0, 1): 5, (1, 0): 2, (1, 1): 3}
+P_BANK = {(0, 0): 6, (0, 1): 7, (1, 0): 0, (1, 1): 1}
+Y_BANK = {(0, 0): 2, (0, 1): 3, (1, 0): 6, (1, 1): 7}
 
 
 def tile_attend_gqa_cap_kernel(tc, qT, kT, vT, vs, offs, out):
@@ -42,147 +57,147 @@ def tile_attend_gqa_cap_kernel(tc, qT, kT, vT, vs, offs, out):
         psum = ctx.enter_context(tc.psum_pool(name="psum", bufs=1))
         units = [(b, m) for b in range(B) for m in range(QT)]
 
-        ROW = 4 * N
-        V_AT = [0, 4 * ROW]
-        Q_AT = [8 * ROW, 11 * ROW]
-        K_AT = 16 * ROW
+        def at(offset, shape, dtype, name):
+            return shared.tile(shape, dtype, name=name, offset=offset, align_bytes=64)
+
+        def aligned(shape, dtype, name):
+            return keep.tile(shape, dtype, name=name, align_bytes=64)
+
+        def bank(number, shape):
+            return psum.tile(shape, F32, name=f"bank{number}")
 
         offsets = keep.tile([P, B * COLS], U16, name="offsets")
         k_raw = [
-            shared.tile([P, 2, c1 - c0], F32, name=f"k_raw{i}", offset=K_AT, align_bytes=64)
-            if i == 2
-            else keep.tile([P, 2, c1 - c0], F32, name=f"k_raw{i}")
-            for i, (u, c0, c1, e) in enumerate(K_CHUNKS)
+            at(K_AT, [P, 2, end - start], F32, f"k_raw{i}")
+            if i == LAST_SCALAR_CAST
+            else keep.tile([P, 2, end - start], F32, name=f"k_raw{i}")
+            for i, (u, start, end, share) in enumerate(K_LOADS)
         ]
         k_pairs = [keep.tile([P, T], U32, name=f"k_pairs{u}") for u in range(2)]
-        v_pool = [shared.tile([P, T], F32, name=f"v_pool{h}", offset=V_AT[h], align_bytes=64) for h in range(VB)]
-        q_raw = [shared.tile([P, PACK, NQ], F32, name=f"q_raw{b}", offset=Q_AT[b], align_bytes=64) for b in range(B)]
+        v_pool = [at(V_AT[h], [P, T], F32, f"v_pool{h}") for h in range(VB)]
+        q_raw = [at(Q_AT[b], [P, PACK, NQ], F32, f"q_raw{b}") for b in range(B)]
         vs_pool = keep.tile([P, T], F32, name="vs_pool")
         vs_row = keep.tile([P, B * N], F32, name="vs_row")
-        vs_col = shared.tile([P, B, PACK], F32, name="vs_col", offset=K_AT, align_bytes=64)
+        vs_col = at(K_AT, [P, B, PACK], F32, "vs_col")
         ident = keep.tile([P, P], F32, name="ident")
         warm = keep.tile([P, 1], F32, name="warm")
         totals = keep.tile([P, B * QT], F32, name="totals")
-        inv = shared.tile([P, B * QT], F32, name="inv", offset=V_AT[1] + 3 * ROW, align_bytes=64)
-        q_packed = [keep.tile([P, NQ, PACK], BF16, name=f"q_packed{b}", align_bytes=64) for b in range(B)]
-        q_codes = [keep.tile([P, NQ], U32, name=f"q_codes{b}", align_bytes=64) for b in range(B)]
-        q_scales = [keep.tile([P, NQ], U8, name=f"q_scales{b}", align_bytes=64) for b in range(B)]
+        inv = at(V_AT[1] + 3 * ROW, [P, B * QT], F32, "inv")
+        q_packed = [aligned([P, NQ, PACK], BF16, f"q_packed{b}") for b in range(B)]
+        q_codes = [aligned([P, NQ], U32, f"q_codes{b}") for b in range(B)]
+        q_scales = [aligned([P, NQ], U8, f"q_scales{b}") for b in range(B)]
         k_words = keep.tile([P, 2, B * N], U32, name="k_words")
-        H = N // 2
         k_packed = {
-            (0, 0): keep.tile([P, H, 2], U32, name="k_packed00", align_bytes=64),
-            (0, 1): keep.tile([P, H, 2], U32, name="k_packed01", align_bytes=64),
-            (1, 0): shared.tile([P, H, 2], U32, name="k_packed10", offset=Q_AT[0], align_bytes=64),
-            (1, 1): shared.tile([P, H, 2], U32, name="k_packed11", offset=Q_AT[1] - ROW + 64, align_bytes=64),
+            (0, 0): aligned([P, HALF, 2], U32, "k_packed00"),
+            (0, 1): aligned([P, HALF, 2], U32, "k_packed01"),
+            (1, 0): at(Q_AT[0], [P, HALF, 2], U32, "k_packed10"),
+            (1, 1): at(Q_AT[1] - ROW + EDGE, [P, HALF, 2], U32, "k_packed11"),
         }
-        k_codes = [keep.tile([P, N], U32, name=f"k_codes{b}", align_bytes=64) for b in range(B)]
+        k_codes = [aligned([P, N], U32, f"k_codes{b}") for b in range(B)]
         k_scales = [
-            keep.tile([P, N], U8, name="k_scales0", align_bytes=64),
-            shared.tile([P, N], U8, name="k_scales1", offset=Q_AT[1] + 64, align_bytes=64),
+            aligned([P, N], U8, "k_scales0"),
+            at(Q_AT[1] + EDGE, [P, N], U8, "k_scales1"),
         ]
-        v_rows = [keep.tile([P, B * N], BF16, name=f"v_rows{h}", align_bytes=64) for h in range(VB)]
+        v_rows = [aligned([P, B * N], BF16, f"v_rows{h}") for h in range(VB)]
         v_packed = [
-            keep.tile([P, VB, P, 2], F32, name="v_packed0", align_bytes=64),
-            shared.tile([P, VB, P, 2], F32, name="v_packed1", offset=V_AT[0] + 3 * ROW, align_bytes=64),
+            aligned([P, VB, P, 2], F32, "v_packed0"),
+            at(V_AT[0] + 3 * ROW, [P, VB, P, 2], F32, "v_packed1"),
         ]
-        v_codes = [keep.tile([P, DV], U32, name=f"v_codes{b}", align_bytes=64) for b in range(B)]
-        v_scales = [keep.tile([P, DV], U8, name=f"v_scales{b}", align_bytes=64) for b in range(B)]
-        w_codes = [keep.tile([P, NQ], U32, name=f"w_codes{b}", align_bytes=64) for b in range(B)]
-        w_scales = [keep.tile([P, NQ], U8, name=f"w_scales{b}", align_bytes=64) for b in range(B)]
-        w_packed = [
-            shared.tile([P, NQ, PACK], BF16, name=f"w_packed{b}", offset=V_AT[1] + b * ROW, align_bytes=64)
-            for b in range(B)
-        ]
+        v_codes = [aligned([P, DV], U32, f"v_codes{b}") for b in range(B)]
+        v_scales = [aligned([P, DV], U8, f"v_scales{b}") for b in range(B)]
+        w_codes = [aligned([P, NQ], U32, f"w_codes{b}") for b in range(B)]
+        w_scales = [aligned([P, NQ], U8, f"w_scales{b}") for b in range(B)]
+        w_packed = [at(V_AT[1] + b * ROW, [P, NQ, PACK], BF16, f"w_packed{b}") for b in range(B)]
         th_of = [
-            shared.tile([P, QT, N], F32, name="th0", offset=Q_AT[1] + 2 * ROW - 64, align_bytes=64),
+            at(Q_AT[1] + 2 * ROW - EDGE, [P, QT, N], F32, "th0"),
             keep.tile([P, QT, N], F32, name="th1"),
         ]
         th = {(b, m): th_of[b][:, m, :] for b, m in units}
-        neg = {
-            (b, m): shared.tile([P, N], F32, name=f"neg{b}{m}", offset=V_AT[0] + (2 * b + m) * ROW, align_bytes=64)
-            for b, m in units
-        }
+        neg = {(b, m): at(V_AT[0] + (QT * b + m) * ROW, [P, N], F32, f"neg{b}{m}") for b, m in units}
         w_planes = keep.tile([P, PACK, P], BF16, name="w_planes")
         low = {u: keep.tile([P, 1], F32, name=f"low{u[0]}{u[1]}") for u in units}
         p = {u: keep.tile([P, PACK, P], F32, name=f"p{u[0]}{u[1]}") for u in units}
         res = {u: keep.tile([P, DV], F32, name=f"res{u[0]}{u[1]}") for u in units}
-        score, wt, vt, acc = {}, {}, {}, {}
+        score, p_turned, v_turned, y = {}, {}, {}, {}
 
-        def quant(codes, scales, packed):
+        def list_of(b):
+            return offsets[:, b * COLS : (b + 1) * COLS]
+
+        def quantise(codes, scales, packed):
             nc.vector.quantize_mx(out=codes.bitcast(FP8X4), scales=scales, in_=packed)
 
-        def interleave_q(b):
-            nc.scalar.copy(
-                q_packed[b][:].rearrange("p (c i) j -> p c j i", i=4), q_raw[b][:].rearrange("p j (c i) -> p c j i", i=4)
-            )
-
-        def quant_q(b):
-            quant(q_codes[b][:], q_scales[b][:], q_packed[b][:].rearrange("p n j -> p (n j)"))
-
-        def gather_vs():
-            nc.vector.tensor_copy(vs_row[:], vs_pool[:].indirect(offsets[:]))
-
-        def turn_vs():
-            for b in range(B):
-                up = psum.tile([P, PACK, P], F32, name=f"bank{4 + b}")
-                for t in range(PACK):
-                    nc.tensor.transpose(up[:, t, :], vs_row[:, b * N + t : (b + 1) * N : PACK], ident[:])
-                nc.scalar.copy(vs_col[:, b, :], up[:, :, 0])
-
-        def cast_k(i):
-            u, c0, c1, share = K_CHUNKS[i]
-            for copy, a, z in ((cast_scalar, 0, share), (nc.vector.tensor_copy, share, c1 - c0)):
-                if a < z:
-                    dst = k_pairs[u][:, c0 + a : c0 + z].bitcast(BF16).rearrange("p (n j) -> p n j", j=2)
-                    copy(dst, k_raw[i][:, :, a:z].rearrange("p j n -> p n j"))
-
-        def cast_scalar(dst, src):
-            nc.scalar.activation(dst, src, ACT.Copy)
-
-        def gather_k(u):
-            nc.vector.tensor_copy(k_words[:, u, :], k_pairs[u][:].indirect(offsets[:]))
-
-        def gather_k_of(u, b):
-            nc.vector.tensor_copy(
-                k_words[:, u, b * N : (b + 1) * N], k_pairs[u][:].indirect(offsets[:, b * COLS : (b + 1) * COLS])
-            )
-
-        def weave_k(copy, word, b, c):
-            cols = slice(b * N + c * H, b * N + (c + 1) * H)
-            copy(k_packed[b, c][:].bitcast(word), k_words[:].bitcast(word)[:, :, cols].rearrange("p u n -> p n u"))
-
-        def quant_k(b, c):
-            cols = slice(c * H, (c + 1) * H)
-            quant(k_codes[b][:, cols], k_scales[b][:, cols], k_packed[b, c][:].rearrange("p n u -> p (n u)").bitcast(BF16))
-
-        def scores(b, m):
-            cols = slice(m * P, (m + 1) * P)
-            s = psum.tile([P, N], F32, name=f"bank{2 * b + m}")
-            score[b, m] = s
+        def mx_product(result, left_codes, left_scales, right_codes, right_scales):
             nc.tensor.matmul_mx(
-                out=s[:],
-                lhsT=q_codes[b][:, cols].bitcast(FP8X4),
-                lhsT_scale=q_scales[b][:, cols],
-                rhs=k_codes[b][:].bitcast(FP8X4),
-                rhs_scale=k_scales[b][:],
+                out=result,
+                lhsT=left_codes.bitcast(FP8X4),
+                lhsT_scale=left_scales,
+                rhs=right_codes.bitcast(FP8X4),
+                rhs_scale=right_scales,
                 start=True,
                 stop=True,
             )
 
-        def squash(*u):
+        def interleave_q(b):
+            nc.scalar.copy(
+                q_packed[b][:].rearrange("p (c i) j -> p c j i", i=4),
+                q_raw[b][:].rearrange("p j (c i) -> p c j i", i=4),
+            )
+
+        def quantise_q(b):
+            quantise(q_codes[b][:], q_scales[b][:], q_packed[b][:].rearrange("p n j -> p (n j)"))
+
+        def turn_vs():
+            for b in range(B):
+                turned = bank(VS_BANK[b], [P, PACK, P])
+                for t in range(PACK):
+                    nc.tensor.transpose(turned[:, t, :], vs_row[:, b * N + t : (b + 1) * N : PACK], ident[:])
+                nc.scalar.copy(vs_col[:, b, :], turned[:, :, 0])
+
+        def cast_on_scalar(dst, src):
+            nc.scalar.activation(dst, src, ACT.Copy)
+
+        def cast_k(i):
+            u, start, end, share = K_LOADS[i]
+            for cast, a, z in ((cast_on_scalar, 0, share), (nc.vector.tensor_copy, share, end - start)):
+                if a < z:
+                    pairs = k_pairs[u][:, start + a : start + z].bitcast(BF16)
+                    cast(
+                        pairs.rearrange("p (n i j) -> p n j i", i=4, j=2),
+                        k_raw[i][:, :, a:z].rearrange("p j (n i) -> p n j i", i=4),
+                    )
+
+        def gather_k(u, b):
+            nc.vector.tensor_copy(k_words[:, u, b * N : (b + 1) * N], k_pairs[u][:].indirect(list_of(b)))
+
+        def weave_k(copy, word, b, half):
+            slots = slice(b * N + half * HALF, b * N + (half + 1) * HALF)
+            copy(
+                k_packed[b, half][:].bitcast(word).rearrange("p (n i) u -> p n u i", i=2),
+                k_words[:].bitcast(word)[:, :, slots].rearrange("p u (n i) -> p n u i", i=2),
+            )
+
+        def quantise_k(b, half):
+            cols = slice(half * HALF, (half + 1) * HALF)
+            packed = k_packed[b, half][:].rearrange("p n u -> p (n u)").bitcast(BF16)
+            quantise(k_codes[b][:, cols], k_scales[b][:, cols], packed)
+
+        def scores(b, m):
+            cols = slice(m * P, (m + 1) * P)
+            score[b, m] = bank(SCORE_BANK[b, m], [P, N])
+            mx_product(score[b, m][:], q_codes[b][:, cols], q_scales[b][:, cols], k_codes[b][:], k_scales[b][:])
+
+        def squash(u):
             nc.scalar.activation(
-                th[u].rearrange("q (t s) -> q t s", t=PACK),
-                score[u][:].rearrange("q (s t) -> q t s", t=PACK),
+                th[u].rearrange("q (t s) -> q s t", t=PACK),
+                score[u][:].rearrange("q (s t) -> q s t", t=PACK),
                 ACT.Tanh,
                 scale=1.0 / CAP,
             )
 
-        def lowest(*u):
-            nc.vector.tensor_scalar(
-                neg[u][:], th[u], -CAP, None, op0=ALU.mult, op1=ALU.min, accum_out=low[u][:]
-            )
+        def lowest(u):
+            nc.vector.tensor_scalar(neg[u][:], th[u], -CAP, None, op0=ALU.mult, op1=ALU.min, accum_out=low[u][:])
 
-        def expo(*u):
+        def expo(u):
             i = units.index(u)
             nc.scalar.activation(
                 p[u][:].rearrange("q t s -> q (t s)"),
@@ -193,76 +208,60 @@ def tile_attend_gqa_cap_kernel(tc, qT, kT, vT, vs, offs, out):
                 accum_out=totals[:, i : i + 1],
             )
 
-        def turn_w(*u):
-            x = psum.tile([P, PACK, P], F32, name=f"bank{6 - 6 * u[0] + u[1]}")
-            wt[u] = x
+        def turn_p(u):
+            p_turned[u] = bank(P_BANK[u], [P, PACK, P])
             for t in range(PACK):
-                nc.tensor.transpose(x[:, t, :], p[u][:, t, :], ident[:])
+                nc.tensor.transpose(p_turned[u][:, t, :], p[u][:, t, :], ident[:])
 
-        def weigh(b, m):
+        def weigh_on_vector(b, m):
             nc.vector.tensor_tensor(
                 w_packed[b][:, m * P : (m + 1) * P, :],
-                wt[b, m][:].rearrange("p t q -> p q t"),
+                p_turned[b, m][:].rearrange("p t q -> p q t"),
                 vs_col[:, b, :].unsqueeze(1).to_broadcast([P, P, PACK]),
                 ALU.mult,
             )
 
-        def weigh_scalar(b, m):
+        def weigh_on_scalar(b, m):
             for t in range(PACK):
-                nc.scalar.activation(w_planes[:, t, :], wt[b, m][:, t, :], ACT.Copy, scale=vs_col[:, b, t : t + 1])
+                nc.scalar.activation(
+                    w_planes[:, t, :], p_turned[b, m][:, t, :], ACT.Copy, scale=vs_col[:, b, t : t + 1]
+                )
             nc.scalar.copy(w_packed[b][:, m * P : (m + 1) * P, :], w_planes[:].rearrange("p t q -> p q t"))
 
-        def quant_w(b, c0, c1):
-            quant(w_codes[b][:, c0:c1], w_scales[b][:, c0:c1], w_packed[b][:, c0:c1, :].rearrange("p n j -> p (n j)"))
+        def quantise_w(b, cols):
+            quantise(w_codes[b][:, cols], w_scales[b][:, cols], w_packed[b][:, cols, :].rearrange("p n j -> p (n j)"))
 
-        def gather_v(h):
-            nc.vector.tensor_copy(v_rows[h][:], v_pool[h][:].indirect(offsets[:]))
-
-        def gather_v_of(h, b):
-            nc.vector.tensor_copy(
-                v_rows[h][:, b * N : (b + 1) * N], v_pool[h][:].indirect(offsets[:, b * COLS : (b + 1) * COLS])
-            )
-
-        def turn_v(h, b, bank):
-            vt[h, b] = psum.tile([P, 2, P], F32, name=f"bank{bank}")
+        def turn_v(h, b):
+            v_turned[h, b] = bank(V_BANK[h, b], [P, 2, P])
             words = v_rows[h][:].bitcast(F32)
             for u in range(2):
-                nc.tensor.transpose(vt[h, b][:, u, :], words[:, b * N // 2 + u : (b + 1) * N // 2 : 2], ident[:])
+                nc.tensor.transpose(v_turned[h, b][:, u, :], words[:, b * HALF + u : (b + 1) * HALF : 2], ident[:])
 
         def pack_v(h, b):
-            nc.scalar.copy(v_packed[b][:, h, :, :], vt[h, b][:].rearrange("p u e -> p e u"))
+            nc.scalar.copy(v_packed[b][:, h, :, :], v_turned[h, b][:].rearrange("p u e -> p e u"))
 
-        def quant_v(b):
-            quant(v_codes[b][:], v_scales[b][:], v_packed[b][:].rearrange("p h e u -> p (h e u)").bitcast(BF16))
+        def quantise_v(b):
+            quantise(v_codes[b][:], v_scales[b][:], v_packed[b][:].rearrange("p h e u -> p (h e u)").bitcast(BF16))
 
         def product(b, m):
             cols = slice(m * P, (m + 1) * P)
-            y = psum.tile([P, DV], F32, name=f"bank{2 + 4 * b + m}")
-            acc[b, m] = y
-            nc.tensor.matmul_mx(
-                out=y[:],
-                lhsT=w_codes[b][:, cols].bitcast(FP8X4),
-                lhsT_scale=w_scales[b][:, cols],
-                rhs=v_codes[b][:].bitcast(FP8X4),
-                rhs_scale=v_scales[b][:],
-                start=True,
-                stop=True,
-            )
+            y[b, m] = bank(Y_BANK[b, m], [P, DV])
+            mx_product(y[b, m][:], w_codes[b][:, cols], w_scales[b][:, cols], v_codes[b][:], v_scales[b][:])
 
-        def finish(b, m, scalar):
-            u = (b, m)
-            i = units.index(u)
-            if scalar:
-                nc.scalar.activation(res[u][:], acc[u][:], ACT.Copy, scale=inv[:, i : i + 1])
+        def finish(b, m):
+            i = units.index((b, m))
+            if (b, m) == units[-1]:
+                nc.vector.tensor_scalar(res[b, m][:], y[b, m][:], inv[:, i : i + 1], None, op0=ALU.mult)
             else:
-                nc.vector.tensor_scalar(res[u][:], acc[u][:], inv[:, i : i + 1], None, op0=ALU.mult)
-            nc.sync.dma_start(out[b, m * P : (m + 1) * P, :], res[u][:])
+                nc.scalar.activation(res[b, m][:], y[b, m][:], ACT.Copy, scale=inv[:, i : i + 1])
+            nc.sync.dma_start(out[b, m * P : (m + 1) * P, :], res[b, m][:])
 
         nc.gpsimd.memset(vs_pool[:, T // 2 : T], 0.0)
         nc.vector.memset(vs_pool[:, 0 : T // 2], 0.0)
+
         k_rows = kT.rearrange("(p u j) n -> u p j n", u=2, j=2)
-        for i, (u, c0, c1, e) in enumerate(K_CHUNKS):
-            nc.sync.dma_start(k_raw[i][:], k_rows[u][:, :, c0:c1])
+        for i, (u, start, end, share) in enumerate(K_LOADS):
+            nc.sync.dma_start(k_raw[i][:], k_rows[u][:, :, start:end])
             if i == 0:
                 nc.sync.dma_start(offsets[:], offs)
                 nc.sync.dma_start(vs_pool[0:1, :], vs[0:1, :])
@@ -270,64 +269,70 @@ def tile_attend_gqa_cap_kernel(tc, qT, kT, vT, vs, offs, out):
             nc.sync.dma_start(q_raw[b][:], qT[b].rearrange("(p j) n -> p j n", j=PACK))
         for h in range(VB):
             nc.sync.dma_start(v_pool[h][:], vT[h * P : (h + 1) * P, :])
+
         nc.vector.memset(warm[:], 0.0)
         nc.scalar.activation(warm[:], warm[:], ACT.Exp)
         make_identity(nc, ident[:])
 
-        cast_k(0)
-        gather_vs()
-        cast_k(1)
-        gather_k(0)
-        for i in range(2, len(K_CHUNKS)):
+        for i in range(len(K_LOADS)):
             cast_k(i)
+            if i == 0:
+                nc.vector.tensor_copy(vs_row[:], vs_pool[:].indirect(offsets[:]))
+            if i == LAST_OF_WINDOW_0:
+                nc.vector.tensor_copy(k_words[:, 0, :], k_pairs[0][:].indirect(offsets[:]))
         turn_vs()
-        gather_k_of(1, 0)
-        gather_k_of(1, 1)
-        interleave_q(0)
-        interleave_q(1)
-        weave_k(nc.vector.tensor_copy, I32, 0, 0)
-        weave_k(nc.vector.tensor_copy, I32, 0, 1)
-        quant_k(0, 0)
-        quant_k(0, 1)
-        quant_q(0)
+
+        for b in range(B):
+            gather_k(1, b)
+        for b in range(B):
+            interleave_q(b)
+        for half in range(2):
+            weave_k(nc.vector.tensor_copy, I32, 0, half)
+        for half in range(2):
+            quantise_k(0, half)
+        quantise_q(0)
         weave_k(nc.scalar.copy, U32, 1, 1)
         weave_k(nc.vector.tensor_copy, I32, 1, 0)
-        quant_q(1)
-        quant_k(1, 0)
-        quant_k(1, 1)
+        quantise_q(1)
+        for half in range(2):
+            quantise_k(1, half)
         for u in units:
             scores(*u)
-            squash(*u)
-        gather_v_of(0, 0)
-        gather_v_of(0, 1)
-        turn_v(0, 0, 4)
-        turn_v(0, 1, 5)
+            squash(u)
+
+        for b in range(B):
+            nc.vector.tensor_copy(v_rows[0][:, b * N : (b + 1) * N], v_pool[0][:].indirect(list_of(b)))
+        for b in range(B):
+            turn_v(0, b)
         pack_v(0, 0)
+
         for u in units:
-            lowest(*u)
-            expo(*u)
-            turn_w(*u)
-        weigh_scalar(0, 0)
+            lowest(u)
+            expo(u)
+            turn_p(u)
+        weigh_on_scalar(0, 0)
         pack_v(0, 1)
-        gather_v(1)
-        turn_v(1, 0, 2)
-        turn_v(1, 1, 3)
-        pack_v(1, 0)
-        pack_v(1, 1)
-        weigh(0, 1)
-        weigh(1, 0)
-        quant_w(0, 0, NQ)
-        quant_v(0)
-        weigh(1, 1)
+
+        nc.vector.tensor_copy(v_rows[1][:], v_pool[1][:].indirect(offsets[:]))
+        for b in range(B):
+            turn_v(1, b)
+        for b in range(B):
+            pack_v(1, b)
+
+        weigh_on_vector(0, 1)
+        weigh_on_vector(1, 0)
+        quantise_w(0, slice(0, NQ))
+        quantise_v(0)
+        weigh_on_vector(1, 1)
         nc.vector.reciprocal(inv[:], totals[:])
-        product(0, 0)
-        product(0, 1)
-        quant_v(1)
-        quant_w(1, 0, P)
-        quant_w(1, P, NQ)
-        finish(0, 0, True)
-        finish(0, 1, True)
-        product(1, 0)
-        product(1, 1)
-        finish(1, 0, True)
-        finish(1, 1, False)
+        for m in range(QT):
+            product(0, m)
+        quantise_v(1)
+        for m in range(QT):
+            quantise_w(1, slice(m * P, (m + 1) * P))
+        for m in range(QT):
+            finish(0, m)
+        for m in range(QT):
+            product(1, m)
+        for m in range(QT):
+            finish(1, m)

@@ -40,6 +40,7 @@ ROW = 4 * N
 EDGE = 64
 V_AT = [0, 4 * ROW]
 Q_AT = [8 * ROW, 11 * ROW]
+W_AT = 15 * ROW
 K_AT = 16 * ROW
 
 SCORE_BANK = {(0, 0): 0, (0, 1): 1, (1, 0): 2, (1, 1): 3}
@@ -82,7 +83,7 @@ def tile_attend_gqa_cap_kernel(tc, qT, kT, vT, vs, offs, out):
         ident = keep.tile([P, P], F32, name="ident")
         warm = keep.tile([P, 1], F32, name="warm")
         totals = keep.tile([P, B * QT], F32, name="totals")
-        inv = at(V_AT[1] + 3 * ROW, [P, B * QT], F32, "inv")
+        inv = keep.tile([P, B * QT], F32, name="inv")
         q_packed = [aligned([P, NQ, PACK], BF16, f"q_packed{b}") for b in range(B)]
         q_codes = [aligned([P, NQ], U32, f"q_codes{b}") for b in range(B)]
         q_scales = [aligned([P, NQ], U8, f"q_scales{b}") for b in range(B)]
@@ -98,7 +99,7 @@ def tile_attend_gqa_cap_kernel(tc, qT, kT, vT, vs, offs, out):
             aligned([P, N], U8, "k_scales0"),
             at(Q_AT[1] + EDGE, [P, N], U8, "k_scales1"),
         ]
-        v_rows = [aligned([P, B * N], BF16, f"v_rows{h}") for h in range(VB)]
+        v_rows = [aligned([P, B * N], BF16, "v_rows0"), at(V_AT[0], [P, B * N], BF16, "v_rows1")]
         v_packed = [
             aligned([P, VB, P, 2], F32, "v_packed0"),
             at(V_AT[0] + 3 * ROW, [P, VB, P, 2], F32, "v_packed1"),
@@ -107,14 +108,20 @@ def tile_attend_gqa_cap_kernel(tc, qT, kT, vT, vs, offs, out):
         v_scales = [aligned([P, DV], U8, f"v_scales{b}") for b in range(B)]
         w_codes = [aligned([P, NQ], U32, f"w_codes{b}") for b in range(B)]
         w_scales = [aligned([P, NQ], U8, f"w_scales{b}") for b in range(B)]
-        w_packed = [at(V_AT[1] + b * ROW, [P, NQ, PACK], BF16, f"w_packed{b}") for b in range(B)]
+        w_packed0 = aligned([P, NQ, PACK], BF16, "w_packed0")
+        w_packed = {
+            (0, 0): w_packed0[:, :P, :],
+            (0, 1): w_packed0[:, P:, :],
+            (1, 0): aligned([P, P, PACK], BF16, "w_packed10")[:],
+            (1, 1): at(W_AT, [P, P, PACK], BF16, "w_packed11")[:],
+        }
         th_of = [
             at(Q_AT[1] + 2 * ROW - EDGE, [P, QT, N], F32, "th0"),
             keep.tile([P, QT, N], F32, name="th1"),
         ]
         th = {(b, m): th_of[b][:, m, :] for b, m in units}
         neg = {(b, m): at(V_AT[0] + (QT * b + m) * ROW, [P, N], F32, f"neg{b}{m}") for b, m in units}
-        w_planes = keep.tile([P, PACK, P], BF16, name="w_planes")
+        w_planes = at(W_AT, [P, PACK, P], BF16, "w_planes")
         low = {u: keep.tile([P, 1], F32, name=f"low{u[0]}{u[1]}") for u in units}
         p = {u: keep.tile([P, PACK, P], F32, name=f"p{u[0]}{u[1]}") for u in units}
         res = {u: keep.tile([P, DV], F32, name=f"res{u[0]}{u[1]}") for u in units}
@@ -215,7 +222,7 @@ def tile_attend_gqa_cap_kernel(tc, qT, kT, vT, vs, offs, out):
 
         def weigh_on_vector(b, m):
             nc.vector.tensor_tensor(
-                w_packed[b][:, m * P : (m + 1) * P, :],
+                w_packed[b, m],
                 p_turned[b, m][:].rearrange("p t q -> p q t"),
                 vs_col[:, b, :].unsqueeze(1).to_broadcast([P, P, PACK]),
                 ALU.mult,
@@ -226,10 +233,13 @@ def tile_attend_gqa_cap_kernel(tc, qT, kT, vT, vs, offs, out):
                 nc.scalar.activation(
                     w_planes[:, t, :], p_turned[b, m][:, t, :], ACT.Copy, scale=vs_col[:, b, t : t + 1]
                 )
-            nc.scalar.copy(w_packed[b][:, m * P : (m + 1) * P, :], w_planes[:].rearrange("p t q -> p q t"))
+            nc.scalar.copy(w_packed[b, m], w_planes[:].rearrange("p t q -> p q t"))
 
-        def quantise_w(b, cols):
-            quantise(w_codes[b][:, cols], w_scales[b][:, cols], w_packed[b][:, cols, :].rearrange("p n j -> p (n j)"))
+        def quantise_w(b, cols, packed):
+            quantise(w_codes[b][:, cols], w_scales[b][:, cols], packed.rearrange("p n j -> p (n j)"))
+
+        def gather_v(h, b):
+            nc.vector.tensor_copy(v_rows[h][:, b * N : (b + 1) * N], v_pool[h][:].indirect(list_of(b)))
 
         def turn_v(h, b):
             v_turned[h, b] = bank(V_BANK[h, b], [P, 2, P])
@@ -301,7 +311,7 @@ def tile_attend_gqa_cap_kernel(tc, qT, kT, vT, vs, offs, out):
             squash(u)
 
         for b in range(B):
-            nc.vector.tensor_copy(v_rows[0][:, b * N : (b + 1) * N], v_pool[0][:].indirect(list_of(b)))
+            gather_v(0, b)
         for b in range(B):
             turn_v(0, b)
         pack_v(0, 0)
@@ -309,27 +319,29 @@ def tile_attend_gqa_cap_kernel(tc, qT, kT, vT, vs, offs, out):
         for u in units:
             lowest(u)
             expo(u)
+        for b in range(B):
+            gather_v(1, b)
+        for u in units[:-1]:
             turn_p(u)
+        turn_v(1, 0)
+        turn_p(units[-1])
+        turn_v(1, 1)
         weigh_on_scalar(0, 0)
-        pack_v(0, 1)
-
-        nc.vector.tensor_copy(v_rows[1][:], v_pool[1][:].indirect(offsets[:]))
-        for b in range(B):
-            turn_v(1, b)
-        for b in range(B):
-            pack_v(1, b)
+        pack_v(1, 0)
+        for h in range(VB):
+            pack_v(h, 1)
 
         weigh_on_vector(0, 1)
         weigh_on_vector(1, 0)
-        quantise_w(0, slice(0, NQ))
+        nc.vector.reciprocal(inv[:], totals[:])
+        quantise_w(0, slice(0, NQ), w_packed0[:])
         quantise_v(0)
         weigh_on_vector(1, 1)
-        nc.vector.reciprocal(inv[:], totals[:])
         for m in range(QT):
             product(0, m)
         quantise_v(1)
         for m in range(QT):
-            quantise_w(1, slice(m * P, (m + 1) * P))
+            quantise_w(1, slice(m * P, (m + 1) * P), w_packed[1, m])
         for m in range(QT):
             finish(0, m)
         for m in range(QT):

@@ -28,13 +28,12 @@ ALU = mybir.AluOpType
 K_LOADS = [
     (0, 0, T // 2, T // 2),
     (0, T // 2, T, 3 * T // 16),
-    (1, 0, T // 2, T // 2),
-    (1, T // 2, 3 * T // 4, 0),
-    (1, 3 * T // 4, 7 * T // 8, 0),
+    (1, 0, T // 2, 11 * T // 32),
+    (1, T // 2, 7 * T // 8, 9 * T // 64),
     (1, 7 * T // 8, T, 0),
 ]
 LAST_OF_WINDOW_0 = 1
-LAST_SCALAR_CAST = 2
+LAST_SCALAR_CAST = 3
 
 ROW = 4 * N
 EDGE = 64
@@ -233,7 +232,10 @@ def tile_attend_gqa_cap_kernel(tc, qT, kT, vT, vs, offs, out):
                 nc.scalar.activation(
                     w_planes[:, t, :], p_turned[b, m][:, t, :], ACT.Copy, scale=vs_col[:, b, t : t + 1]
                 )
-            nc.scalar.copy(w_packed[b, m], w_planes[:].rearrange("p t q -> p q t"))
+            nc.scalar.copy(
+                w_packed[b, m].rearrange("p (c i) t -> p c t i", i=4),
+                w_planes[:].rearrange("p t (c i) -> p c t i", i=4),
+            )
 
         def quantise_w(b, cols, packed):
             quantise(w_codes[b][:, cols], w_scales[b][:, cols], packed.rearrange("p n j -> p (n j)"))

@@ -98,7 +98,9 @@ def tile_attend_gqa_cap_kernel(tc, qT, kT, vT, vs, offs, out):
             aligned([P, N], U8, "k_scales0"),
             at(Q_AT[1] + EDGE, [P, N], U8, "k_scales1"),
         ]
-        v_rows = [aligned([P, B * N], BF16, "v_rows0"), at(V_AT[0], [P, B * N], BF16, "v_rows1")]
+        v_rows = {(0, b): aligned([P, N], BF16, f"v_rows0{b}") for b in range(B)}
+        for b in range(B):
+            v_rows[1, b] = at(V_AT[0] + QT * b * ROW, [P, N], BF16, f"v_rows1{b}")
         v_packed = [
             aligned([P, VB, P, 2], F32, "v_packed0"),
             at(V_AT[0] + 3 * ROW, [P, VB, P, 2], F32, "v_packed1"),
@@ -121,9 +123,9 @@ def tile_attend_gqa_cap_kernel(tc, qT, kT, vT, vs, offs, out):
         th = {(b, m): th_of[b][:, m, :] for b, m in units}
         neg = {(b, m): at(V_AT[0] + (QT * b + m) * ROW, [P, N], F32, f"neg{b}{m}") for b, m in units}
         w_planes = at(W_AT, [P, PACK, P], BF16, "w_planes")
-        low = {u: keep.tile([P, 1], F32, name=f"low{u[0]}{u[1]}") for u in units}
-        p = {u: keep.tile([P, PACK, P], F32, name=f"p{u[0]}{u[1]}") for u in units}
-        res = {u: keep.tile([P, DV], F32, name=f"res{u[0]}{u[1]}") for u in units}
+        low = {(b, m): keep.tile([P, 1], F32, name=f"low{b}{m}") for b, m in units}
+        p = {(b, m): keep.tile([P, PACK, P], F32, name=f"p{b}{m}") for b, m in units}
+        res = {(b, m): keep.tile([P, DV], F32, name=f"res{b}{m}") for b, m in units}
         score, p_turned, v_turned, y = {}, {}, {}, {}
 
         def list_of(b):
@@ -192,32 +194,34 @@ def tile_attend_gqa_cap_kernel(tc, qT, kT, vT, vs, offs, out):
             score[b, m] = bank(SCORE_BANK[b, m], [P, N])
             mx_product(score[b, m][:], q_codes[b][:, cols], q_scales[b][:, cols], k_codes[b][:], k_scales[b][:])
 
-        def squash(u):
+        def squash(unit):
             nc.scalar.activation(
-                th[u].rearrange("q (t s) -> q s t", t=PACK),
-                score[u][:].rearrange("q (s t) -> q s t", t=PACK),
+                th[unit].rearrange("q (t s) -> q s t", t=PACK),
+                score[unit][:].rearrange("q (s t) -> q s t", t=PACK),
                 ACT.Tanh,
                 scale=1.0 / CAP,
             )
 
-        def lowest(u):
-            nc.vector.tensor_scalar(neg[u][:], th[u], -CAP, None, op0=ALU.mult, op1=ALU.min, accum_out=low[u][:])
+        def lowest(unit):
+            nc.vector.tensor_scalar(
+                neg[unit][:], th[unit], -CAP, None, op0=ALU.mult, op1=ALU.min, accum_out=low[unit][:]
+            )
 
-        def expo(u):
-            i = units.index(u)
+        def expo(unit):
+            i = units.index(unit)
             nc.scalar.activation(
-                p[u][:].rearrange("q t s -> q (t s)"),
-                neg[u][:],
+                p[unit][:].rearrange("q t s -> q (t s)"),
+                neg[unit][:],
                 ACT.Exp,
-                bias=low[u][:],
+                bias=low[unit][:],
                 scale=-1.0,
                 accum_out=totals[:, i : i + 1],
             )
 
-        def turn_p(u):
-            p_turned[u] = bank(P_BANK[u], [P, PACK, P])
+        def turn_p(unit):
+            p_turned[unit] = bank(P_BANK[unit], [P, PACK, P])
             for t in range(PACK):
-                nc.tensor.transpose(p_turned[u][:, t, :], p[u][:, t, :], ident[:])
+                nc.tensor.transpose(p_turned[unit][:, t, :], p[unit][:, t, :], ident[:])
 
         def weigh_on_vector(b, m):
             nc.vector.tensor_tensor(
@@ -241,13 +245,13 @@ def tile_attend_gqa_cap_kernel(tc, qT, kT, vT, vs, offs, out):
             quantise(w_codes[b][:, cols], w_scales[b][:, cols], packed.rearrange("p n j -> p (n j)"))
 
         def gather_v(h, b):
-            nc.vector.tensor_copy(v_rows[h][:, b * N : (b + 1) * N], v_pool[h][:].indirect(list_of(b)))
+            nc.vector.tensor_copy(v_rows[h, b][:], v_pool[h][:].indirect(list_of(b)))
 
         def turn_v(h, b):
             v_turned[h, b] = bank(V_BANK[h, b], [P, 2, P])
-            words = v_rows[h][:].bitcast(F32)
+            words = v_rows[h, b][:].bitcast(F32)
             for u in range(2):
-                nc.tensor.transpose(v_turned[h, b][:, u, :], words[:, b * HALF + u : (b + 1) * HALF : 2], ident[:])
+                nc.tensor.transpose(v_turned[h, b][:, u, :], words[:, u:HALF:2], ident[:])
 
         def pack_v(h, b):
             nc.scalar.copy(v_packed[b][:, h, :, :], v_turned[h, b][:].rearrange("p u e -> p e u"))
@@ -308,9 +312,9 @@ def tile_attend_gqa_cap_kernel(tc, qT, kT, vT, vs, offs, out):
         quantise_q(1)
         for half in range(2):
             quantise_k(1, half)
-        for u in units:
-            scores(*u)
-            squash(u)
+        for unit in units:
+            scores(*unit)
+            squash(unit)
 
         for b in range(B):
             gather_v(0, b)
@@ -318,13 +322,13 @@ def tile_attend_gqa_cap_kernel(tc, qT, kT, vT, vs, offs, out):
             turn_v(0, b)
         pack_v(0, 0)
 
-        for u in units:
-            lowest(u)
-            expo(u)
+        for unit in units:
+            lowest(unit)
+            expo(unit)
         for b in range(B):
             gather_v(1, b)
-        for u in units[:-1]:
-            turn_p(u)
+        for unit in units[:-1]:
+            turn_p(unit)
         turn_v(1, 0)
         turn_p(units[-1])
         turn_v(1, 1)

@@ -37,16 +37,16 @@ LAST_SCALAR_CAST = 3
 
 ROW = 4 * N
 EDGE = 64
-V_AT = [0, 4 * ROW]
+NEG_AT = 0
+TH_AT = ROW
 Q_AT = [8 * ROW, 11 * ROW]
-W_AT = 15 * ROW
 K_AT = 16 * ROW
 
 SCORE_BANK = {(0, 0): 0, (0, 1): 1, (1, 0): 2, (1, 1): 3}
 VS_BANK = [4, 5]
-V_BANK = {(0, 0): 4, (0, 1): 5, (1, 0): 2, (1, 1): 3}
+V_BANK = {(0, 0): 4, (1, 0): 5, (0, 1): 2, (1, 1): 3}
 P_BANK = {(0, 0): 6, (0, 1): 7, (1, 0): 0, (1, 1): 1}
-Y_BANK = {(0, 0): 2, (0, 1): 3, (1, 0): 6, (1, 1): 7}
+Y_BANK = {(0, 0): 4, (0, 1): 5, (1, 0): 6, (1, 1): 7}
 
 
 def tile_attend_gqa_cap_kernel(tc, qT, kT, vT, vs, offs, out):
@@ -74,13 +74,12 @@ def tile_attend_gqa_cap_kernel(tc, qT, kT, vT, vs, offs, out):
             for i, (u, start, end, share) in enumerate(K_LOADS)
         ]
         k_pairs = [keep.tile([P, T], U32, name=f"k_pairs{u}") for u in range(2)]
-        v_pool = [at(V_AT[h], [P, T], F32, f"v_pool{h}") for h in range(VB)]
+        v_pool = [keep.tile([P, T], F32, name=f"v_pool{h}") for h in range(VB)]
         q_raw = [at(Q_AT[b], [P, PACK, NQ], F32, f"q_raw{b}") for b in range(B)]
         vs_pool = keep.tile([P, T], F32, name="vs_pool")
         vs_row = keep.tile([P, B * N], F32, name="vs_row")
         vs_col = at(K_AT, [P, B, PACK], F32, "vs_col")
         ident = keep.tile([P, P], F32, name="ident")
-        warm = keep.tile([P, 1], F32, name="warm")
         totals = keep.tile([P, B * QT], F32, name="totals")
         inv = keep.tile([P, B * QT], F32, name="inv")
         q_packed = [aligned([P, NQ, PACK], BF16, f"q_packed{b}") for b in range(B)]
@@ -98,31 +97,24 @@ def tile_attend_gqa_cap_kernel(tc, qT, kT, vT, vs, offs, out):
             aligned([P, N], U8, "k_scales0"),
             at(Q_AT[1] + EDGE, [P, N], U8, "k_scales1"),
         ]
-        v_rows = {(0, b): aligned([P, N], BF16, f"v_rows0{b}") for b in range(B)}
-        for b in range(B):
-            v_rows[1, b] = at(V_AT[0] + QT * b * ROW, [P, N], BF16, f"v_rows1{b}")
-        v_packed = [
-            aligned([P, VB, P, 2], F32, "v_packed0"),
-            at(V_AT[0] + 3 * ROW, [P, VB, P, 2], F32, "v_packed1"),
-        ]
+        v_rows = {
+            (0, 0): aligned([P, N], BF16, "v_rows00"),
+            (1, 0): at(NEG_AT, [P, N], BF16, "v_rows10"),
+            (0, 1): at(TH_AT, [P, N], BF16, "v_rows01"),
+            (1, 1): at(TH_AT + ROW // 2, [P, N], BF16, "v_rows11"),
+        }
+        v_packed = [aligned([P, VB, P, 2], F32, f"v_packed{b}") for b in range(B)]
         v_codes = [aligned([P, DV], U32, f"v_codes{b}") for b in range(B)]
         v_scales = [aligned([P, DV], U8, f"v_scales{b}") for b in range(B)]
         w_codes = [aligned([P, NQ], U32, f"w_codes{b}") for b in range(B)]
         w_scales = [aligned([P, NQ], U8, f"w_scales{b}") for b in range(B)]
-        w_packed0 = aligned([P, NQ, PACK], BF16, "w_packed0")
-        w_packed = {
-            (0, 0): w_packed0[:, :P, :],
-            (0, 1): w_packed0[:, P:, :],
-            (1, 0): aligned([P, P, PACK], BF16, "w_packed10")[:],
-            (1, 1): at(W_AT, [P, P, PACK], BF16, "w_packed11")[:],
-        }
-        th_of = [
-            at(Q_AT[1] + 2 * ROW - EDGE, [P, QT, N], F32, "th0"),
-            keep.tile([P, QT, N], F32, name="th1"),
-        ]
-        th = {(b, m): th_of[b][:, m, :] for b, m in units}
-        neg = {(b, m): at(V_AT[0] + (QT * b + m) * ROW, [P, N], F32, f"neg{b}{m}") for b, m in units}
-        w_planes = at(W_AT, [P, PACK, P], BF16, "w_planes")
+        w_packed = [aligned([P, NQ, PACK], BF16, f"w_packed{b}") for b in range(B)]
+        th_first = at(Q_AT[1] + 2 * ROW - EDGE, [P, QT, N], F32, "th_first")
+        th = {(0, m): th_first[:, m, :] for m in range(QT)}
+        th[1, 0] = keep.tile([P, N], F32, name="th10")[:]
+        th[1, 1] = at(TH_AT, [P, N], F32, "th_last")[:]
+        neg = {(b, m): keep.tile([P, N], F32, name=f"neg{b}{m}") for b, m in units[1:]}
+        neg[units[0]] = at(NEG_AT, [P, N], F32, "neg_first")
         low = {(b, m): keep.tile([P, 1], F32, name=f"low{b}{m}") for b, m in units}
         p = {(b, m): keep.tile([P, PACK, P], F32, name=f"p{b}{m}") for b, m in units}
         res = {(b, m): keep.tile([P, DV], F32, name=f"res{b}{m}") for b, m in units}
@@ -161,12 +153,12 @@ def tile_attend_gqa_cap_kernel(tc, qT, kT, vT, vs, offs, out):
                     nc.tensor.transpose(turned[:, t, :], vs_row[:, b * N + t : (b + 1) * N : PACK], ident[:])
                 nc.scalar.copy(vs_col[:, b, :], turned[:, :, 0])
 
-        def cast_on_scalar(dst, src):
+        def copy_on_scalar(dst, src):
             nc.scalar.activation(dst, src, ACT.Copy)
 
         def cast_k(i):
             u, start, end, share = K_LOADS[i]
-            for cast, a, z in ((cast_on_scalar, 0, share), (nc.vector.tensor_copy, share, end - start)):
+            for cast, a, z in ((copy_on_scalar, 0, share), (nc.vector.tensor_copy, share, end - start)):
                 if a < z:
                     pairs = k_pairs[u][:, start + a : start + z].bitcast(BF16)
                     cast(
@@ -223,29 +215,19 @@ def tile_attend_gqa_cap_kernel(tc, qT, kT, vT, vs, offs, out):
             for t in range(PACK):
                 nc.tensor.transpose(p_turned[unit][:, t, :], p[unit][:, t, :], ident[:])
 
-        def weigh_on_vector(b, m):
+        def weigh(b, m):
             nc.vector.tensor_tensor(
-                w_packed[b, m],
+                w_packed[b][:, m * P : (m + 1) * P, :],
                 p_turned[b, m][:].rearrange("p t q -> p q t"),
                 vs_col[:, b, :].unsqueeze(1).to_broadcast([P, P, PACK]),
                 ALU.mult,
             )
 
-        def weigh_on_scalar(b, m):
-            for t in range(PACK):
-                nc.scalar.activation(
-                    w_planes[:, t, :], p_turned[b, m][:, t, :], ACT.Copy, scale=vs_col[:, b, t : t + 1]
-                )
-            nc.scalar.copy(
-                w_packed[b, m].rearrange("p (c i) t -> p c t i", i=4),
-                w_planes[:].rearrange("p t (c i) -> p c t i", i=4),
-            )
+        def quantise_w(b, cols):
+            quantise(w_codes[b][:, cols], w_scales[b][:, cols], w_packed[b][:, cols, :].rearrange("p n j -> p (n j)"))
 
-        def quantise_w(b, cols, packed):
-            quantise(w_codes[b][:, cols], w_scales[b][:, cols], packed.rearrange("p n j -> p (n j)"))
-
-        def gather_v(h, b):
-            nc.vector.tensor_copy(v_rows[h, b][:], v_pool[h][:].indirect(list_of(b)))
+        def gather_v(copy, h, b):
+            copy(v_rows[h, b][:], v_pool[h][:].indirect(list_of(b)))
 
         def turn_v(h, b):
             v_turned[h, b] = bank(V_BANK[h, b], [P, 2, P])
@@ -256,8 +238,10 @@ def tile_attend_gqa_cap_kernel(tc, qT, kT, vT, vs, offs, out):
         def pack_v(h, b):
             nc.scalar.copy(v_packed[b][:, h, :, :], v_turned[h, b][:].rearrange("p u e -> p e u"))
 
-        def quantise_v(b):
-            quantise(v_codes[b][:], v_scales[b][:], v_packed[b][:].rearrange("p h e u -> p (h e u)").bitcast(BF16))
+        def quantise_v(b, blocks):
+            cols = slice(blocks.start * P, blocks.stop * P)
+            packed = v_packed[b][:, blocks, :, :].rearrange("p h e u -> p (h e u)").bitcast(BF16)
+            quantise(v_codes[b][:, cols], v_scales[b][:, cols], packed)
 
         def product(b, m):
             cols = slice(m * P, (m + 1) * P)
@@ -285,9 +269,6 @@ def tile_attend_gqa_cap_kernel(tc, qT, kT, vT, vs, offs, out):
             nc.sync.dma_start(q_raw[b][:], qT[b].rearrange("(p j) n -> p j n", j=PACK))
         for h in range(VB):
             nc.sync.dma_start(v_pool[h][:], vT[h * P : (h + 1) * P, :])
-
-        nc.vector.memset(warm[:], 0.0)
-        nc.scalar.activation(warm[:], warm[:], ACT.Exp)
         make_identity(nc, ident[:])
 
         for i in range(len(K_LOADS)):
@@ -316,38 +297,36 @@ def tile_attend_gqa_cap_kernel(tc, qT, kT, vT, vs, offs, out):
             scores(*unit)
             squash(unit)
 
-        for b in range(B):
-            gather_v(0, b)
-        for b in range(B):
-            turn_v(0, b)
-        pack_v(0, 0)
-
+        gather_v(nc.vector.tensor_copy, 0, 0)
         for unit in units:
             lowest(unit)
             expo(unit)
-        for b in range(B):
-            gather_v(1, b)
-        for unit in units[:-1]:
+        gather_v(nc.vector.tensor_copy, 1, 0)
+        for h in range(VB):
+            gather_v(copy_on_scalar, h, 1)
+        turn_v(0, 0)
+        for unit in units[:QT]:
             turn_p(unit)
         turn_v(1, 0)
-        turn_p(units[-1])
-        turn_v(1, 1)
-        weigh_on_scalar(0, 0)
-        pack_v(1, 0)
+        for unit in units[QT:]:
+            turn_p(unit)
         for h in range(VB):
-            pack_v(h, 1)
+            turn_v(h, 1)
+        for b in range(B):
+            for h in range(VB):
+                pack_v(h, b)
 
-        weigh_on_vector(0, 1)
-        weigh_on_vector(1, 0)
+        for unit in units[:-1]:
+            weigh(*unit)
         nc.vector.reciprocal(inv[:], totals[:])
-        quantise_w(0, slice(0, NQ), w_packed0[:])
-        quantise_v(0)
-        weigh_on_vector(1, 1)
+        quantise_w(0, slice(0, NQ))
+        weigh(*units[-1])
+        quantise_v(0, slice(0, VB))
         for m in range(QT):
             product(0, m)
-        quantise_v(1)
-        for m in range(QT):
-            quantise_w(1, slice(m * P, (m + 1) * P), w_packed[1, m])
+        quantise_w(1, slice(0, NQ))
+        for h in range(VB):
+            quantise_v(1, slice(h, h + 1))
         for m in range(QT):
             finish(0, m)
         for m in range(QT):

from contextlib import ExitStack

import concourse.mybir as mybir
from concourse.masks import make_identity

B, N, T, D, DV, NQ = 2, 512, 2048, 512, 256, 256
P = 128
PACK = 4
CAP = 2.0
QT = NQ // P
VB = DV // P
COLS = N // 16
HALF = N // 2

FLOPS = 2 * B * NQ * N * (D + DV)
BYTES = 4 * (B * D * NQ + D * T + DV * T + T + B * NQ * DV) + 2 * P * B * COLS

F32 = mybir.dt.float32
BF16 = mybir.dt.bfloat16
I32 = mybir.dt.int32
U32 = mybir.dt.uint32
U16 = mybir.dt.uint16
U8 = mybir.dt.uint8
FP8X4 = mybir.dt.float8_e4m3fn_x4
ACT = mybir.ActivationFunctionType
ALU = mybir.AluOpType

K_LOADS = [
    (0, 0, T // 2, T // 2),
    (0, T // 2, T, 3 * T // 16),
    (1, 0, T // 2, 11 * T // 32),
    (1, T // 2, 7 * T // 8, 9 * T // 64),
    (1, 7 * T // 8, T, 0),
]
LAST_OF_WINDOW_0 = 1
LAST_SCALAR_CAST = 3

ROW = 4 * N
EDGE = 64
NEG_AT = 0
TH_AT = ROW
Q_AT = [8 * ROW, 11 * ROW]
K_AT = 16 * ROW

SCORE_BANK = {(0, 0): 0, (0, 1): 1, (1, 0): 2, (1, 1): 3}
VS_BANK = [4, 5]
V_BANK = {(0, 0): 4, (1, 0): 5, (0, 1): 2, (1, 1): 3}
P_BANK = {(0, 0): 6, (0, 1): 7, (1, 0): 0, (1, 1): 1}
Y_BANK = {(0, 0): 4, (0, 1): 5, (1, 0): 6, (1, 1): 7}


def tile_attend_gqa_cap_kernel(tc, qT, kT, vT, vs, offs, out):
    nc = tc.nc
    with ExitStack() as ctx:
        keep = ctx.enter_context(tc.tile_pool(name="keep", bufs=1))
        shared = ctx.enter_context(tc.tile_pool(name="shared", bufs=1))
        psum = ctx.enter_context(tc.psum_pool(name="psum", bufs=1))
        units = [(b, m) for b in range(B) for m in range(QT)]

        def at(offset, shape, dtype, name):
            return shared.tile(shape, dtype, name=name, offset=offset, align_bytes=64)

        def aligned(shape, dtype, name):
            return keep.tile(shape, dtype, name=name, align_bytes=64)

        def bank(number, shape):
            return psum.tile(shape, F32, name=f"bank{number}")

        offsets = keep.tile([P, B * COLS], U16, name="offsets")
        k_raw = [
            at(K_AT, [P, 2, end - start], F32, f"k_raw{i}")
            if i == LAST_SCALAR_CAST
            else keep.tile([P, 2, end - start], F32, name=f"k_raw{i}")
            for i, (u, start, end, share) in enumerate(K_LOADS)
        ]
        k_pairs = [keep.tile([P, T], U32, name=f"k_pairs{u}") for u in range(2)]
        v_pool = [keep.tile([P, T], F32, name=f"v_pool{h}") for h in range(VB)]
        q_raw = [at(Q_AT[b], [P, PACK, NQ], F32, f"q_raw{b}") for b in range(B)]
        vs_pool = keep.tile([P, T], F32, name="vs_pool")
        vs_row = keep.tile([P, B * N], F32, name="vs_row")
        vs_col = at(K_AT, [P, B, PACK], F32, "vs_col")
        ident = keep.tile([P, P], F32, name="ident")
        totals = keep.tile([P, B * QT], F32, name="totals")
        inv = keep.tile([P, B * QT], F32, name="inv")
        q_packed = [aligned([P, NQ, PACK], BF16, f"q_packed{b}") for b in range(B)]
        q_codes = [aligned([P, NQ], U32, f"q_codes{b}") for b in range(B)]
        q_scales = [aligned([P, NQ], U8, f"q_scales{b}") for b in range(B)]
        k_words = keep.tile([P, 2, B * N], U32, name="k_words")
        k_packed = {
            (0, 0): aligned([P, HALF, 2], U32, "k_packed00"),
            (0, 1): aligned([P, HALF, 2], U32, "k_packed01"),
            (1, 0): at(Q_AT[0], [P, HALF, 2], U32, "k_packed10"),
            (1, 1): at(Q_AT[1] - ROW + EDGE, [P, HALF, 2], U32, "k_packed11"),
        }
        k_codes = [aligned([P, N], U32, f"k_codes{b}") for b in range(B)]
        k_scales = [
            aligned([P, N], U8, "k_scales0"),
            at(Q_AT[1] + EDGE, [P, N], U8, "k_scales1"),
        ]
        v_rows = {
            (0, 0): aligned([P, N], BF16, "v_rows00"),
            (1, 0): at(NEG_AT, [P, N], BF16, "v_rows10"),
            (0, 1): at(TH_AT, [P, N], BF16, "v_rows01"),
            (1, 1): at(TH_AT + ROW // 2, [P, N], BF16, "v_rows11"),
        }
        v_packed = [aligned([P, VB, P, 2], F32, f"v_packed{b}") for b in range(B)]
        v_codes = [aligned([P, DV], U32, f"v_codes{b}") for b in range(B)]
        v_scales = [aligned([P, DV], U8, f"v_scales{b}") for b in range(B)]
        w_codes = [aligned([P, NQ], U32, f"w_codes{b}") for b in range(B)]
        w_scales = [aligned([P, NQ], U8, f"w_scales{b}") for b in range(B)]
        w_packed = [aligned([P, NQ, PACK], BF16, f"w_packed{b}") for b in range(B)]
        th_first = at(Q_AT[1] + 2 * ROW - EDGE, [P, QT, N], F32, "th_first")
        th = {(0, m): th_first[:, m, :] for m in range(QT)}
        th[1, 0] = keep.tile([P, N], F32, name="th10")[:]
        th[1, 1] = at(TH_AT, [P, N], F32, "th_last")[:]
        neg = {(b, m): keep.tile([P, N], F32, name=f"neg{b}{m}") for b, m in units[1:]}
        neg[units[0]] = at(NEG_AT, [P, N], F32, "neg_first")
        low = {(b, m): keep.tile([P, 1], F32, name=f"low{b}{m}") for b, m in units}
        p = {(b, m): keep.tile([P, PACK, P], F32, name=f"p{b}{m}") for b, m in units}
        res = {(b, m): keep.tile([P, DV], F32, name=f"res{b}{m}") for b, m in units}
        score, p_turned, v_turned, y = {}, {}, {}, {}

        def list_of(b):
            return offsets[:, b * COLS : (b + 1) * COLS]

        def quantise(codes, scales, packed):
            nc.vector.quantize_mx(out=codes.bitcast(FP8X4), scales=scales, in_=packed)

        def mx_product(result, left_codes, left_scales, right_codes, right_scales):
            nc.tensor.matmul_mx(
                out=result,
                lhsT=left_codes.bitcast(FP8X4),
                lhsT_scale=left_scales,
                rhs=right_codes.bitcast(FP8X4),
                rhs_scale=right_scales,
                start=True,
                stop=True,
            )

        def interleave_q(b):
            nc.scalar.copy(
                q_packed[b][:].rearrange("p (c i) j -> p c j i", i=4),
                q_raw[b][:].rearrange("p j (c i) -> p c j i", i=4),
            )

        def quantise_q(b):
            quantise(q_codes[b][:], q_scales[b][:], q_packed[b][:].rearrange("p n j -> p (n j)"))

        def turn_vs():
            for b in range(B):
                turned = bank(VS_BANK[b], [P, PACK, P])
                for t in range(PACK):
                    nc.tensor.transpose(turned[:, t, :], vs_row[:, b * N + t : (b + 1) * N : PACK], ident[:])
                nc.scalar.copy(vs_col[:, b, :], turned[:, :, 0])

        def copy_on_scalar(dst, src):
            nc.scalar.activation(dst, src, ACT.Copy)

        def cast_k(i):
            u, start, end, share = K_LOADS[i]
            for cast, a, z in ((copy_on_scalar, 0, share), (nc.vector.tensor_copy, share, end - start)):
                if a < z:
                    pairs = k_pairs[u][:, start + a : start + z].bitcast(BF16)
                    cast(
                        pairs.rearrange("p (n i j) -> p n j i", i=4, j=2),
                        k_raw[i][:, :, a:z].rearrange("p j (n i) -> p n j i", i=4),
                    )

        def gather_k(u, b):
            nc.vector.tensor_copy(k_words[:, u, b * N : (b + 1) * N], k_pairs[u][:].indirect(list_of(b)))

        def weave_k(copy, word, b, half):
            slots = slice(b * N + half * HALF, b * N + (half + 1) * HALF)
            copy(
                k_packed[b, half][:].bitcast(word).rearrange("p (n i) u -> p n u i", i=2),
                k_words[:].bitcast(word)[:, :, slots].rearrange("p u (n i) -> p n u i", i=2),
            )

        def quantise_k(b, half):
            cols = slice(half * HALF, (half + 1) * HALF)
            packed = k_packed[b, half][:].rearrange("p n u -> p (n u)").bitcast(BF16)
            quantise(k_codes[b][:, cols], k_scales[b][:, cols], packed)

        def scores(b, m):
            cols = slice(m * P, (m + 1) * P)
            score[b, m] = bank(SCORE_BANK[b, m], [P, N])
            mx_product(score[b, m][:], q_codes[b][:, cols], q_scales[b][:, cols], k_codes[b][:], k_scales[b][:])

        def squash(unit):
            nc.scalar.activation(
                th[unit].rearrange("q (t s) -> q s t", t=PACK),
                score[unit][:].rearrange("q (s t) -> q s t", t=PACK),
                ACT.Tanh,
                scale=1.0 / CAP,
            )

        def lowest(unit):
            nc.vector.tensor_scalar(
                neg[unit][:], th[unit], -CAP, None, op0=ALU.mult, op1=ALU.min, accum_out=low[unit][:]
            )

        def expo(unit):
            i = units.index(unit)
            nc.scalar.activation(
                p[unit][:].rearrange("q t s -> q (t s)"),
                neg[unit][:],
                ACT.Exp,
                bias=low[unit][:],
                scale=-1.0,
                accum_out=totals[:, i : i + 1],
            )

        def turn_p(unit):
            p_turned[unit] = bank(P_BANK[unit], [P, PACK, P])
            for t in range(PACK):
                nc.tensor.transpose(p_turned[unit][:, t, :], p[unit][:, t, :], ident[:])

        def weigh(b, m):
            nc.vector.tensor_tensor(
                w_packed[b][:, m * P : (m + 1) * P, :],
                p_turned[b, m][:].rearrange("p t q -> p q t"),
                vs_col[:, b, :].unsqueeze(1).to_broadcast([P, P, PACK]),
                ALU.mult,
            )

        def quantise_w(b, cols):
            quantise(w_codes[b][:, cols], w_scales[b][:, cols], w_packed[b][:, cols, :].rearrange("p n j -> p (n j)"))

        def gather_v(copy, h, b):
            copy(v_rows[h, b][:], v_pool[h][:].indirect(list_of(b)))

        def turn_v(h, b):
            v_turned[h, b] = bank(V_BANK[h, b], [P, 2, P])
            words = v_rows[h, b][:].bitcast(F32)
            for u in range(2):
                nc.tensor.transpose(v_turned[h, b][:, u, :], words[:, u:HALF:2], ident[:])

        def pack_v(h, b):
            nc.scalar.copy(v_packed[b][:, h, :, :], v_turned[h, b][:].rearrange("p u e -> p e u"))

        def quantise_v(b, blocks):
            cols = slice(blocks.start * P, blocks.stop * P)
            packed = v_packed[b][:, blocks, :, :].rearrange("p h e u -> p (h e u)").bitcast(BF16)
            quantise(v_codes[b][:, cols], v_scales[b][:, cols], packed)

        def product(b, m):
            cols = slice(m * P, (m + 1) * P)
            y[b, m] = bank(Y_BANK[b, m], [P, DV])
            mx_product(y[b, m][:], w_codes[b][:, cols], w_scales[b][:, cols], v_codes[b][:], v_scales[b][:])

        def finish(b, m):
            i = units.index((b, m))
            if (b, m) == units[-1]:
                nc.vector.tensor_scalar(res[b, m][:], y[b, m][:], inv[:, i : i + 1], None, op0=ALU.mult)
            else:
                nc.scalar.activation(res[b, m][:], y[b, m][:], ACT.Copy, scale=inv[:, i : i + 1])
            nc.sync.dma_start(out[b, m * P : (m + 1) * P, :], res[b, m][:])

        nc.gpsimd.memset(vs_pool[:, T // 2 : T], 0.0)
        nc.vector.memset(vs_pool[:, 0 : T // 2], 0.0)

        k_rows = kT.rearrange("(p u j) n -> u p j n", u=2, j=2)
        for i, (u, start, end, share) in enumerate(K_LOADS):
            nc.sync.dma_start(k_raw[i][:], k_rows[u][:, :, start:end])
            if i == 0:
                nc.sync.dma_start(offsets[:], offs)
                nc.sync.dma_start(vs_pool[0:1, :], vs[0:1, :])
        for b in range(B):
            nc.sync.dma_start(q_raw[b][:], qT[b].rearrange("(p j) n -> p j n", j=PACK))
        for h in range(VB):
            nc.sync.dma_start(v_pool[h][:], vT[h * P : (h + 1) * P, :])
        make_identity(nc, ident[:])

        for i in range(len(K_LOADS)):
            cast_k(i)
            if i == 0:
                nc.vector.tensor_copy(vs_row[:], vs_pool[:].indirect(offsets[:]))
            if i == LAST_OF_WINDOW_0:
                nc.vector.tensor_copy(k_words[:, 0, :], k_pairs[0][:].indirect(offsets[:]))
        turn_vs()

        for b in range(B):
            gather_k(1, b)
        for b in range(B):
            interleave_q(b)
        for half in range(2):
            weave_k(nc.vector.tensor_copy, I32, 0, half)
        for half in range(2):
            quantise_k(0, half)
        quantise_q(0)
        weave_k(nc.scalar.copy, U32, 1, 1)
        weave_k(nc.vector.tensor_copy, I32, 1, 0)
        quantise_q(1)
        for half in range(2):
            quantise_k(1, half)
        for unit in units:
            scores(*unit)
            squash(unit)

        gather_v(nc.vector.tensor_copy, 0, 0)
        for unit in units:
            lowest(unit)
            expo(unit)
        gather_v(nc.vector.tensor_copy, 1, 0)
        for h in range(VB):
            gather_v(copy_on_scalar, h, 1)
        turn_v(0, 0)
        for unit in units[:QT]:
            turn_p(unit)
        turn_v(1, 0)
        for unit in units[QT:]:
            turn_p(unit)
        for h in range(VB):
            turn_v(h, 1)
        for b in range(B):
            for h in range(VB):
                pack_v(h, b)

        for unit in units[:-1]:
            weigh(*unit)
        nc.vector.reciprocal(inv[:], totals[:])
        quantise_w(0, slice(0, NQ))
        weigh(*units[-1])
        quantise_v(0, slice(0, VB))
        for m in range(QT):
            product(0, m)
        quantise_w(1, slice(0, NQ))
        for h in range(VB):
            quantise_v(1, slice(h, h + 1))
        for m in range(QT):
            finish(0, m)
        for m in range(QT):
            product(1, m)
        for m in range(QT):
            finish(1, m)
